import numpy as np
import ml_dtypes


def mxq(x, axis, fmt="e4m3"):
    dtype, down = {"e4m3": (ml_dtypes.float8_e4m3fn, 7), "e5m2": (ml_dtypes.float8_e5m2, 14)}[fmt]
    v = np.moveaxis(np.asarray(x, np.float32).astype(ml_dtypes.bfloat16).astype(np.float64), axis, -1)
    blocks = v.reshape(v.shape[:-1] + (-1, 32))
    amax = np.abs(blocks).max(-1, keepdims=True)
    byte = np.maximum(np.where(amax > 0, np.frexp(amax)[1] - 1 + 127, 0) - down, 1)
    scale = np.exp2(byte - 127.0)
    codes = (blocks / scale).astype(np.float32).astype(dtype).astype(np.float64)
    return np.moveaxis((codes * scale).reshape(v.shape), -1, axis)


WIDE = False


def mx_kscale(k):
    if not WIDE:
        return np.ones(k)
    levels = np.array([10, -10, 5, -5, 0])
    if k % 512:
        return np.exp2(np.random.permutation(np.resize(levels, k // 32))).repeat(32)
    a = np.empty((k // 512, 16))
    for p in range(k // 512):
        a[p, :8] = np.random.permutation(np.resize(levels, 8))
        for g in range(8):
            far = levels[np.abs(levels - a[p, g]) >= 10]
            a[p, g + 8] = far[np.random.randint(len(far))]
    return np.exp2(a.ravel()).repeat(32)


def f64(x):
    return np.asarray(x).astype(np.float64)


def striped(idx):
    return np.tile(idx.reshape(-1, 16).T, (8, 1)).astype(np.uint16)


def unstriped(offs):
    return offs[:16].T.reshape(-1).astype(np.int64)


def pack_weight(w):
    k, n = w.shape
    w = f64(np.asarray(w, np.float32).astype(ml_dtypes.bfloat16)).reshape(k // 32, 32, n)
    amax = np.abs(w).max(1)
    byte = np.clip(np.where(amax > 0, np.frexp(amax)[1] - 1 + 127 - 7, 1), 1, 254)
    scaled = (w * np.exp2(127.0 - byte)[:, None, :]).reshape(k, n).astype(np.float32)
    words = np.ascontiguousarray(scaled.reshape(k // 512, 128, 4, n).transpose(0, 1, 3, 2)).astype(ml_dtypes.float8_e4m3fn).view(np.uint8)
    return words, np.ascontiguousarray(byte.astype(np.uint8).reshape(k // 512, 16, n))


def unpack_weight(words, scales):
    g, p, n, _ = words.shape
    vals = np.ascontiguousarray(words).view(ml_dtypes.float8_e4m3fn).astype(np.float64) * np.repeat(np.exp2(scales.astype(np.float64) - 127.0), 8, axis=1)[..., None]
    return vals.transpose(0, 1, 3, 2).reshape(g * 512, n)


def planes(y):
    n, m = y.shape
    v = y.astype(np.float32).astype(ml_dtypes.bfloat16).astype(np.float64).reshape(n // 32, 32, m)
    top = np.abs(v).max(1)
    byte = np.clip(np.where(top > 0, np.frexp(top)[1] - 1 + 127 - 7, 1), 1, 254)
    codes = (v * np.exp2(127.0 - byte)[:, None, :]).reshape(n, m).astype(np.float32).astype(ml_dtypes.float8_e4m3fn).view(np.uint8)
    words = codes.reshape(n // 512, 128, 4, m).transpose(0, 1, 3, 2)
    return np.ascontiguousarray(words), np.ascontiguousarray(byte.astype(np.uint8).reshape(n // 512, 16, m))


def sigmoid(v):
    return 1.0 / (1.0 + np.exp(-np.maximum(v, -700.0)))


K, T, S, V, H, N = 512, 1024, 512, 256, 512, 512


def setup_inputs():
    n = np.random.standard_normal
    s = mx_kscale(K)[:, None]
    u = mx_kscale(H)
    near = np.random.permutation(S)
    packed_xT = pack_weight(n((K, T)) * s)
    packed_w1 = pack_weight(n((K, N)) / np.sqrt(K) / s)
    packed_w2 = pack_weight(n((K, N)) / np.sqrt(K) / s)
    packed_w4 = pack_weight(n((H, N)) / np.sqrt(H) / u[:, None])
    return {
        "x_words": packed_xT[0],
        "x_scales": packed_xT[1],
        "w1_words": packed_w1[0],
        "w1_scales": packed_w1[1],
        "w2_words": packed_w2[0],
        "w2_scales": packed_w2[1],
        "w3": (n((K, H)) / np.sqrt(K) / s * u).astype(np.float32),
        "w4_words": packed_w4[0],
        "w4_scales": packed_w4[1],
        "offs": striped(np.random.permutation(T)[:S]),
        "tgt": striped(np.random.permutation(T)[:V]),
        "pos1": striped(near[:V]),
        "pos2": striped(near[V:]),
    }


def reference(x_words, x_scales, w1_words, w1_scales, w2_words, w2_scales, w3, w4_words, w4_scales, offs, tgt, pos1, pos2):
    xq = unpack_weight(x_words, x_scales)[:, unstriped(offs)]
    e = unpack_weight(w2_words, w2_scales).T @ xq
    x_tgt = unpack_weight(x_words, x_scales)[:, unstriped(tgt)]
    y = unpack_weight(w1_words, w1_scales).T @ x_tgt
    a0 = sigmoid(e[:, unstriped(pos1)] * y)
    h = mxq(f64(w3), 0, "e4m3").T @ xq
    a1 = sigmoid(e[:, unstriped(pos2)] * y)
    z = a0 * h[:, unstriped(pos1)] + a1 * h[:, unstriped(pos2)]
    out_0 = unpack_weight(w4_words, w4_scales).T @ mxq(z, 0, "e4m3")
    return (out_0,) + planes(out_0)

@@ -1,0 +1,217 @@
+from contextlib import ExitStack
+
+import concourse.mybir as mybir
+
+K, T, S, V, H, N = 512, 1024, 512, 256, 512, 512
+FLOPS = 2 * K * (N * V + N * S + H * S) + 2 * H * N * V
+
+F32 = mybir.dt.float32
+BF16 = mybir.dt.bfloat16
+I32 = mybir.dt.int32
+U32 = mybir.dt.uint32
+U16 = mybir.dt.uint16
+U8 = mybir.dt.uint8
+FP8X4 = mybir.dt.float8_e4m3fn_x4
+MULT = mybir.AluOpType.mult
+ADD = mybir.AluOpType.add
+SIGMOID = mybir.ActivationFunctionType.Sigmoid
+
+P = 128
+PACK = 4
+QUADS = 4
+CHUNKS = ((0, 128), (128, 256))
+
+
+def load_words(queue, tile, words):
+    queue.dma_start(out=tile[:].bitcast(I32), in_=words[0].rearrange("p n t -> p (n t)").bitcast(I32))
+
+
+def load_scales(queue, tile, scales, row, quads=range(QUADS)):
+    for q in quads:
+        queue.dma_start(
+            out=tile[32 * q + row : 32 * q + row + 4, :].bitcast(I32),
+            in_=scales[0, 4 * q : 4 * q + 4, :].bitcast(I32),
+        )
+
+
+def deal(nc, dealt, raw):
+    nc.vector.tensor_copy(
+        out=dealt[:].rearrange("p (t c i) -> p c t i", t=PACK, i=4),
+        in_=raw[:].rearrange("p (c i t) -> p c t i", t=PACK, i=4),
+    )
+
+
+def tile_picked_zdin_sigmoid_po_kernel(
+    tc, x_words, x_scales, w1_words, w1_scales, w2_words, w2_scales, w3, w4_words, w4_scales,
+    offs, tgt, pos1, pos2, out_0, out_1, out_2,
+):
+    nc = tc.nc
+    with ExitStack() as ctx:
+        lists = ctx.enter_context(tc.tile_pool(name="lists", bufs=1))
+        keep = ctx.enter_context(tc.tile_pool(name="keep", bufs=1))
+        psum = ctx.enter_context(tc.psum_pool(name="psum", bufs=2))
+
+        offs_sb = lists.tile([P, S // 16], U16, name="offs_sb")
+        tgt_sb = lists.tile([P, V // 16], U16, name="tgt_sb")
+        pos_sb = [lists.tile([P, V // 16], U16, name=f"pos_sb{d}") for d in range(2)]
+
+        def sb(name, shape, dtype):
+            return keep.tile(shape, dtype, name=name, align_bytes=64)
+
+        x_word = sb("x_word", [P, T], U32)
+        x_scale = sb("x_scale", [P, T], U8)
+        w1_raw = sb("w1_raw", [P, N], U32)
+        w2_raw = sb("w2_raw", [P, N], U32)
+        w4_raw = sb("w4_raw", [P, N], U32)
+        w12_scale_raw = sb("w12_scale_raw", [P, N], U8)
+        w4_scale_raw = sb("w4_scale_raw", [P, N], U8)
+        w3_raw = [sb(f"w3_raw{u}", [P, PACK, H // 2], F32) for u in range(2)]
+        warm = sb("warm", [P, 8], F32)
+        warm_out = sb("warm_out", [P, 8], F32)
+
+        nc.gpsimd.memset(x_scale[:].bitcast(I32), 0)
+        nc.gpsimd.memset(w12_scale_raw[:].bitcast(I32), 0)
+        nc.vector.memset(warm[:], 0.0)
+        nc.vector.memset(w4_scale_raw[:].bitcast(I32), 0)
+        nc.scalar.activation(out=warm_out[:], in_=warm[:], func=SIGMOID)
+
+        load_words(nc.sync, x_word, x_words)
+        nc.sync.dma_start(tgt_sb[:], tgt)
+        nc.sync.dma_start(offs_sb[:], offs)
+        load_words(nc.sync, w1_raw, w1_words)
+        load_scales(nc.sync, x_scale, x_scales, 0)
+        load_scales(nc.gpsimd, w12_scale_raw, w2_scales, 4, range(3, 4))
+        load_words(nc.sync, w2_raw, w2_words)
+        load_scales(nc.sync, w12_scale_raw, w1_scales, 0)
+        load_scales(nc.sync, w12_scale_raw, w2_scales, 4, range(3))
+        w3_rows = w3.rearrange("(p j) c -> p j c", j=PACK)
+        for u in range(2):
+            nc.sync.dma_start(out=w3_raw[u][:], in_=w3_rows[:, :, u * (H // 2) : (u + 1) * (H // 2)])
+        nc.sync.dma_start(pos_sb[0][:], pos1)
+        nc.sync.dma_start(pos_sb[1][:], pos2)
+        load_words(nc.sync, w4_raw, w4_words)
+        load_scales(nc.sync, w4_scale_raw, w4_scales, 0)
+
+        tgt_word = sb("tgt_word", [P, V], U32)
+        tgt_scale = sb("tgt_scale", [P, V], U8)
+        hist_word = sb("hist_word", [P, S], U32)
+        hist_scale = sb("hist_scale", [P, S], U8)
+        w1_word = sb("w1_word", [P, N], U32)
+        w2_word = sb("w2_word", [P, N], U32)
+        w4_word = sb("w4_word", [P, N], U32)
+        w12_scale = sb("w12_scale", [P, N], U8)
+        w4_scale = sb("w4_scale", [P, N], U8)
+
+        nc.vector.tensor_copy(out=tgt_word[:], in_=x_word[:].indirect(tgt_sb[:]))
+        nc.vector.tensor_copy(out=tgt_scale[:], in_=x_scale[:].indirect(tgt_sb[:]))
+        deal(nc, w1_word, w1_raw)
+        nc.vector.tensor_copy(out=hist_word[:], in_=x_word[:].indirect(offs_sb[:]))
+        deal(nc, w12_scale, w12_scale_raw)
+        deal(nc, w2_word, w2_raw)
+        nc.vector.tensor_copy(out=hist_scale[:], in_=x_scale[:].indirect(offs_sb[:]))
+
+        def product(acc, word, scale, row, t, rhs_word, rhs_scale):
+            cols = slice(P * t, P * (t + 1))
+            nc.tensor.matmul_mx(
+                out=acc, lhsT=word[:, cols].bitcast(FP8X4), lhsT_scale=scale[row:P, cols],
+                rhs=rhs_word.bitcast(FP8X4), rhs_scale=rhs_scale, start=True, stop=True,
+            )
+
+        y_sb = [sb(f"y_sb{u}", [P, 2, V], F32) for u in range(2)]
+        for u in range(2):
+            y_ps = psum.tile([P, 2, V], F32, name="y_ps")
+            for s in range(2):
+                product(y_ps[:, s, :], w1_word, w12_scale, 0, 2 * u + s, tgt_word[:], tgt_scale[:])
+            nc.scalar.copy(out=y_sb[u][:], in_=y_ps[:])
+
+        e_sb = [sb(f"e_sb{t}", [P, S], F32) for t in range(PACK)]
+        for t in range(PACK):
+            e_ps = psum.tile([P, S], F32, name="e_ps")
+            product(e_ps[:], w2_word, w12_scale, 4, t, hist_word[:], hist_scale[:])
+            nc.scalar.copy(out=e_sb[t][:], in_=e_ps[:])
+
+        w3_bf = sb("w3_bf", [P, PACK, P, PACK], BF16)
+        for u, copy in enumerate((nc.vector.tensor_copy, nc.scalar.copy)):
+            copy(
+                out=w3_bf[:, :, u * (P // 2) : (u + 1) * (P // 2), :].rearrange("p t m j -> p m t j"),
+                in_=w3_raw[u][:].rearrange("p j (m t) -> p m t j", t=PACK),
+            )
+
+        logit = [sb(f"logit{t}", [P, 2, V], F32) for t in range(PACK)]
+        gate = [sb(f"gate{t}", [P, 2, V], F32) for t in range(PACK)]
+        w3_word = sb("w3_word", [P, H], U32)
+        w3_scale = sb("w3_scale", [P, H], U8)
+        h_sb = [sb(f"h_sb{t}", [P, S], F32) for t in range(PACK)]
+        for t in range(PACK):
+            for d in range(2):
+                nc.vector.tensor_tensor(
+                    out=logit[t][:, d, :], in0=e_sb[t][:].indirect(pos_sb[d][:]), in1=y_sb[t // 2][:, t % 2, :], op=MULT
+                )
+            if t == 2:
+                nc.vector.quantize_mx(
+                    out=w3_word[:].bitcast(FP8X4), scales=w3_scale[:], in_=w3_bf[:].rearrange("p t m j -> p (t m j)")
+                )
+            nc.scalar.activation(out=gate[t][:], in_=logit[t][:], func=SIGMOID)
+        deal(nc, w4_word, w4_raw)
+        deal(nc, w4_scale, w4_scale_raw)
+        for t in range(PACK):
+            h_ps = psum.tile([P, S], F32, name="h_ps")
+            product(h_ps[:], w3_word, w3_scale, 0, t, hist_word[:], hist_scale[:])
+            nc.scalar.copy(out=h_sb[t][:], in_=h_ps[:])
+
+        out_rows = out_0.rearrange("(p t) v -> p t v", t=PACK)
+        out_words = out_1[0].rearrange("p v t -> p (v t)").bitcast(I32)
+        out_scale = sb("out_scale", [P, V], U8)
+        pending = []
+
+        def hand_on(c, lo, hi, out_bf):
+            out_word = sb(f"out_word{c}", [P, hi - lo], U32)
+            nc.vector.quantize_mx(
+                out=out_word[:].bitcast(FP8X4), scales=out_scale[:, lo:hi], in_=out_bf[:].rearrange("p v t -> p (v t)")
+            )
+            nc.sync.dma_start(out=out_words[:, lo:hi], in_=out_word[:].bitcast(I32))
+
+        for c, (lo, hi) in enumerate(CHUNKS):
+            width = hi - lo
+            term = [sb(f"term{c}_{d}", [P, PACK, width], F32) for d in range(2)]
+            for t in range(PACK):
+                for d in range(2):
+                    nc.vector.tensor_tensor(
+                        out=term[d][:, t, :], in0=h_sb[t][:].indirect(pos_sb[d][:, lo // 16 : hi // 16]),
+                        in1=gate[t][:, d, lo:hi], op=MULT,
+                    )
+            z_bf = sb(f"z_bf{c}", [P, width, PACK], BF16)
+            nc.vector.tensor_tensor(
+                out=z_bf[:].rearrange("p (c i) t -> p c t i", i=2),
+                in0=term[0][:].rearrange("p t (c i) -> p c t i", i=2),
+                in1=term[1][:].rearrange("p t (c i) -> p c t i", i=2),
+                op=ADD,
+            )
+            for args in pending:
+                hand_on(*args)
+            pending = []
+            z_word = sb(f"z_word{c}", [P, width], U32)
+            z_scale = sb(f"z_scale{c}", [P, width], U8)
+            nc.vector.quantize_mx(
+                out=z_word[:].bitcast(FP8X4), scales=z_scale[:], in_=z_bf[:].rearrange("p v t -> p (v t)")
+            )
+            out_ps = psum.tile([P, PACK, width], F32, name="out_ps")
+            for t in range(PACK):
+                product(out_ps[:, t, :], w4_word, w4_scale, 0, t, z_word[:], z_scale[:])
+            out_sb = sb(f"out_sb{c}", [P, PACK, width], F32)
+            nc.scalar.copy(out=out_sb[:], in_=out_ps[:])
+            nc.sync.dma_start(out=out_rows[:, :, lo:hi], in_=out_sb[:])
+            out_bf = sb(f"out_bf{c}", [P, width, PACK], BF16)
+            copy = nc.vector.tensor_copy if c == len(CHUNKS) - 1 else nc.scalar.copy
+            copy(
+                out=out_bf[:].rearrange("p (c i) t -> p c t i", i=2),
+                in_=out_sb[:].rearrange("p t (c i) -> p c t i", i=2),
+            )
+            pending.append((c, lo, hi, out_bf))
+        for args in pending:
+            hand_on(*args)
+        for q in range(QUADS):
+            queue = nc.sync if q % 2 == 0 else nc.scalar
+            queue.dma_start(
+                out=out_2[0, 4 * q : 4 * q + 4, :].bitcast(I32), in_=out_scale[32 * q : 32 * q + 4, :].bitcast(I32)
+            )

@@ -19,7 +19,6 @@ SIGMOID = mybir.ActivationFunctionType.Sigmoid
 P = 128
 PACK = 4
 QUADS = 4
-CHUNKS = ((0, 128), (128, 256))
 
 
 def load_words(queue, tile, words):
@@ -55,8 +54,8 @@ def tile_picked_zdin_sigmoid_po_kernel(
         tgt_sb = lists.tile([P, V // 16], U16, name="tgt_sb")
         pos_sb = [lists.tile([P, V // 16], U16, name=f"pos_sb{d}") for d in range(2)]
 
-        def sb(name, shape, dtype):
-            return keep.tile(shape, dtype, name=name, align_bytes=64)
+        def sb(name, shape, dtype, tag=""):
+            return keep.tile(shape, dtype, name=name, tag=tag, align_bytes=64)
 
         x_word = sb("x_word", [P, T], U32)
         x_scale = sb("x_scale", [P, T], U8)
@@ -70,23 +69,24 @@ def tile_picked_zdin_sigmoid_po_kernel(
         warm_out = sb("warm_out", [P, 8], F32)
 
         nc.gpsimd.memset(x_scale[:].bitcast(I32), 0)
-        nc.gpsimd.memset(w12_scale_raw[:].bitcast(I32), 0)
-        nc.vector.memset(warm[:], 0.0)
+        nc.gpsimd.memset(warm[:], 0.0)
+        nc.vector.memset(w12_scale_raw[:].bitcast(I32), 0)
         nc.vector.memset(w4_scale_raw[:].bitcast(I32), 0)
-        nc.scalar.activation(out=warm_out[:], in_=warm[:], func=SIGMOID)
 
-        load_words(nc.sync, x_word, x_words)
         nc.sync.dma_start(tgt_sb[:], tgt)
+        load_scales(nc.sync, x_scale, x_scales, 0, range(2))
+        load_scales(nc.scalar, x_scale, x_scales, 0, range(2, 4))
+        nc.scalar.activation(out=warm_out[:], in_=warm[:], func=SIGMOID)
         nc.sync.dma_start(offs_sb[:], offs)
+        load_words(nc.sync, x_word, x_words)
         load_words(nc.sync, w1_raw, w1_words)
-        load_scales(nc.sync, x_scale, x_scales, 0)
-        load_scales(nc.gpsimd, w12_scale_raw, w2_scales, 4, range(3, 4))
         load_words(nc.sync, w2_raw, w2_words)
-        load_scales(nc.sync, w12_scale_raw, w1_scales, 0)
-        load_scales(nc.sync, w12_scale_raw, w2_scales, 4, range(3))
         w3_rows = w3.rearrange("(p j) c -> p j c", j=PACK)
-        for u in range(2):
-            nc.sync.dma_start(out=w3_raw[u][:], in_=w3_rows[:, :, u * (H // 2) : (u + 1) * (H // 2)])
+        nc.sync.dma_start(out=w3_raw[0][:], in_=w3_rows[:, :, : H // 2])
+        load_scales(nc.sync, w12_scale_raw, w1_scales, 0)
+        load_scales(nc.sync, w12_scale_raw, w2_scales, 4, range(2))
+        load_scales(nc.gpsimd, w12_scale_raw, w2_scales, 4, range(2, 4))
+        nc.sync.dma_start(out=w3_raw[1][:], in_=w3_rows[:, :, H // 2 :])
         nc.sync.dma_start(pos_sb[0][:], pos1)
         nc.sync.dma_start(pos_sb[1][:], pos2)
         load_words(nc.sync, w4_raw, w4_words)
@@ -102,13 +102,13 @@ def tile_picked_zdin_sigmoid_po_kernel(
         w12_scale = sb("w12_scale", [P, N], U8)
         w4_scale = sb("w4_scale", [P, N], U8)
 
-        nc.vector.tensor_copy(out=tgt_word[:], in_=x_word[:].indirect(tgt_sb[:]))
         nc.vector.tensor_copy(out=tgt_scale[:], in_=x_scale[:].indirect(tgt_sb[:]))
-        deal(nc, w1_word, w1_raw)
-        nc.vector.tensor_copy(out=hist_word[:], in_=x_word[:].indirect(offs_sb[:]))
-        deal(nc, w12_scale, w12_scale_raw)
-        deal(nc, w2_word, w2_raw)
         nc.vector.tensor_copy(out=hist_scale[:], in_=x_scale[:].indirect(offs_sb[:]))
+        nc.vector.tensor_copy(out=tgt_word[:], in_=x_word[:].indirect(tgt_sb[:]))
+        deal(nc, w1_word, w1_raw)
+        deal(nc, w2_word, w2_raw)
+        deal(nc, w12_scale, w12_scale_raw)
+        nc.vector.tensor_copy(out=hist_word[:], in_=x_word[:].indirect(offs_sb[:]))
 
         def product(acc, word, scale, row, t, rhs_word, rhs_scale):
             cols = slice(P * t, P * (t + 1))
@@ -117,99 +117,127 @@ def tile_picked_zdin_sigmoid_po_kernel(
                 rhs=rhs_word.bitcast(FP8X4), rhs_scale=rhs_scale, start=True, stop=True,
             )
 
-        y_sb = [sb(f"y_sb{u}", [P, 2, V], F32) for u in range(2)]
-        for u in range(2):
-            y_ps = psum.tile([P, 2, V], F32, name="y_ps")
-            for s in range(2):
-                product(y_ps[:, s, :], w1_word, w12_scale, 0, 2 * u + s, tgt_word[:], tgt_scale[:])
-            nc.scalar.copy(out=y_sb[u][:], in_=y_ps[:])
-
-        e_sb = [sb(f"e_sb{t}", [P, S], F32) for t in range(PACK)]
-        for t in range(PACK):
-            e_ps = psum.tile([P, S], F32, name="e_ps")
-            product(e_ps[:], w2_word, w12_scale, 4, t, hist_word[:], hist_scale[:])
-            nc.scalar.copy(out=e_sb[t][:], in_=e_ps[:])
-
+        y_sb = [sb(f"y_sb{t}", [P, V], F32) for t in range(PACK)]
+        e_sb = {}
+        h_sb = [sb(f"h_sb{t}", [P, S], F32) for t in range(PACK)]
+        logit = {}
+        gate = [sb(f"gate{t}", [P, 2, V], F32) for t in range(PACK)]
+        term = [sb(f"term{d}", [P, PACK, V], F32) for d in range(2)]
         w3_bf = sb("w3_bf", [P, PACK, P, PACK], BF16)
-        for u, copy in enumerate((nc.vector.tensor_copy, nc.scalar.copy)):
+        w3_word = sb("w3_word", [P, H], U32)
+        w3_scale = sb("w3_scale", [P, H], U8)
+
+        def round_w3(u, copy):
             copy(
-                out=w3_bf[:, :, u * (P // 2) : (u + 1) * (P // 2), :].rearrange("p t m j -> p m t j"),
+                out=w3_bf[:, :, 64 * u : 64 * (u + 1), :].rearrange("p t m j -> p m t j"),
                 in_=w3_raw[u][:].rearrange("p j (m t) -> p m t j", t=PACK),
             )
 
-        logit = [sb(f"logit{t}", [P, 2, V], F32) for t in range(PACK)]
-        gate = [sb(f"gate{t}", [P, 2, V], F32) for t in range(PACK)]
-        w3_word = sb("w3_word", [P, H], U32)
-        w3_scale = sb("w3_scale", [P, H], U8)
-        h_sb = [sb(f"h_sb{t}", [P, S], F32) for t in range(PACK)]
-        for t in range(PACK):
+        def targets(t):
+            acc = psum.tile([P, V], F32, name="y_ps")
+            product(acc[:], w1_word, w12_scale, 0, t, tgt_word[:], tgt_scale[:])
+            nc.scalar.copy(out=y_sb[t][:], in_=acc[:])
+
+        def history(result, word, scale, row, t, lo=0, hi=S, copy=nc.scalar.copy):
+            acc = psum.tile([P, hi - lo], F32, name="hist_ps", bufs=4)
+            product(acc[:], word, scale, row, t, hist_word[:, lo:hi], hist_scale[:, lo:hi])
+            copy(out=result[t][:, lo:hi], in_=acc[:])
+
+        def logits(t, tag=""):
+            logit[t] = sb(f"logit{t}", [P, 2, V], F32, tag)
             for d in range(2):
                 nc.vector.tensor_tensor(
-                    out=logit[t][:, d, :], in0=e_sb[t][:].indirect(pos_sb[d][:]), in1=y_sb[t // 2][:, t % 2, :], op=MULT
+                    out=logit[t][:, d, :], in0=e_sb[t][:].indirect(pos_sb[d][:]), in1=y_sb[t][:], op=MULT
                 )
-            if t == 2:
-                nc.vector.quantize_mx(
-                    out=w3_word[:].bitcast(FP8X4), scales=w3_scale[:], in_=w3_bf[:].rearrange("p t m j -> p (t m j)")
-                )
+
+        def gates(t):
             nc.scalar.activation(out=gate[t][:], in_=logit[t][:], func=SIGMOID)
+
+        def weigh(t, d, lo, hi):
+            nc.vector.tensor_tensor(
+                out=term[d][:, t, lo:hi], in0=h_sb[t][:].indirect(pos_sb[d][:, lo // 16 : hi // 16]),
+                in1=gate[t][:, d, lo:hi], op=MULT,
+            )
+
+        def keys(t, tag=""):
+            e_sb[t] = sb(f"e_sb{t}", [P, S], F32, tag)
+            history(e_sb, w2_word, w12_scale, 4, t)
+            targets(t)
+
+        round_w3(0, nc.scalar.copy)
+        e_sb[0] = sb("e_sb0", [P, S], F32)
+        history(e_sb, w2_word, w12_scale, 4, 0, 0, S // 2)
+        history(e_sb, w2_word, w12_scale, 4, 0, S // 2, S, nc.vector.tensor_copy)
+        targets(0)
+        round_w3(1, nc.vector.tensor_copy)
+        nc.vector.quantize_mx(
+            out=w3_word[:].bitcast(FP8X4), scales=w3_scale[:], in_=w3_bf[:].rearrange("p t m j -> p (t m j)")
+        )
+        logits(0)
+        for t in range(1, PACK):
+            keys(t)
+            logits(t)
         deal(nc, w4_word, w4_raw)
         deal(nc, w4_scale, w4_scale_raw)
         for t in range(PACK):
-            h_ps = psum.tile([P, S], F32, name="h_ps")
-            product(h_ps[:], w3_word, w3_scale, 0, t, hist_word[:], hist_scale[:])
-            nc.scalar.copy(out=h_sb[t][:], in_=h_ps[:])
+            gates(t)
+            history(h_sb, w3_word, w3_scale, 0, t)
+        for t in range(PACK - 1):
+            for d in range(2):
+                weigh(t, d, 0, V)
 
         out_rows = out_0.rearrange("(p t) v -> p t v", t=PACK)
         out_words = out_1[0].rearrange("p v t -> p (v t)").bitcast(I32)
         out_scale = sb("out_scale", [P, V], U8)
-        pending = []
+        half = V // 2
+        z_bf = [sb(f"z_bf{c}", [P, half, PACK], BF16) for c in range(2)]
+        out_bf = [sb(f"out_bf{c}", [P, half, PACK], BF16) for c in range(2)]
 
-        def hand_on(c, lo, hi, out_bf):
-            out_word = sb(f"out_word{c}", [P, hi - lo], U32)
-            nc.vector.quantize_mx(
-                out=out_word[:].bitcast(FP8X4), scales=out_scale[:, lo:hi], in_=out_bf[:].rearrange("p v t -> p (v t)")
-            )
-            nc.sync.dma_start(out=out_words[:, lo:hi], in_=out_word[:].bitcast(I32))
-
-        for c, (lo, hi) in enumerate(CHUNKS):
-            width = hi - lo
-            term = [sb(f"term{c}_{d}", [P, PACK, width], F32) for d in range(2)]
-            for t in range(PACK):
-                for d in range(2):
-                    nc.vector.tensor_tensor(
-                        out=term[d][:, t, :], in0=h_sb[t][:].indirect(pos_sb[d][:, lo // 16 : hi // 16]),
-                        in1=gate[t][:, d, lo:hi], op=MULT,
-                    )
-            z_bf = sb(f"z_bf{c}", [P, width, PACK], BF16)
+        def add_terms(c):
+            cols = slice(c * half, (c + 1) * half)
             nc.vector.tensor_tensor(
-                out=z_bf[:].rearrange("p (c i) t -> p c t i", i=2),
-                in0=term[0][:].rearrange("p t (c i) -> p c t i", i=2),
-                in1=term[1][:].rearrange("p t (c i) -> p c t i", i=2),
+                out=z_bf[c][:].rearrange("p (c i) t -> p c t i", i=2),
+                in0=term[0][:, :, cols].rearrange("p t (c i) -> p c t i", i=2),
+                in1=term[1][:, :, cols].rearrange("p t (c i) -> p c t i", i=2),
                 op=ADD,
             )
-            for args in pending:
-                hand_on(*args)
-            pending = []
-            z_word = sb(f"z_word{c}", [P, width], U32)
-            z_scale = sb(f"z_scale{c}", [P, width], U8)
+
+        def last_product(c, copy):
+            z_word = sb(f"z_word{c}", [P, half], U32)
+            z_scale = sb(f"z_scale{c}", [P, half], U8)
             nc.vector.quantize_mx(
-                out=z_word[:].bitcast(FP8X4), scales=z_scale[:], in_=z_bf[:].rearrange("p v t -> p (v t)")
+                out=z_word[:].bitcast(FP8X4), scales=z_scale[:], in_=z_bf[c][:].rearrange("p v t -> p (v t)")
             )
-            out_ps = psum.tile([P, PACK, width], F32, name="out_ps")
-            for t in range(PACK):
-                product(out_ps[:, t, :], w4_word, w4_scale, 0, t, z_word[:], z_scale[:])
-            out_sb = sb(f"out_sb{c}", [P, PACK, width], F32)
-            nc.scalar.copy(out=out_sb[:], in_=out_ps[:])
-            nc.sync.dma_start(out=out_rows[:, :, lo:hi], in_=out_sb[:])
-            out_bf = sb(f"out_bf{c}", [P, width, PACK], BF16)
-            copy = nc.vector.tensor_copy if c == len(CHUNKS) - 1 else nc.scalar.copy
+            out_sb = sb(f"out_sb{c}", [P, PACK, half], F32)
+            for u, empty in enumerate((nc.scalar.copy, copy)):
+                out_ps = psum.tile([P, 2, half], F32, name="out_ps")
+                for s in range(2):
+                    product(out_ps[:, s, :], w4_word, w4_scale, 0, 2 * u + s, z_word[:], z_scale[:])
+                empty(out=out_sb[:, 2 * u : 2 * u + 2, :], in_=out_ps[:])
+            nc.sync.dma_start(out=out_rows[:, :, c * half : (c + 1) * half], in_=out_sb[:])
             copy(
-                out=out_bf[:].rearrange("p (c i) t -> p c t i", i=2),
+                out=out_bf[c][:].rearrange("p (c i) t -> p c t i", i=2),
                 in_=out_sb[:].rearrange("p t (c i) -> p c t i", i=2),
             )
-            pending.append((c, lo, hi, out_bf))
-        for args in pending:
-            hand_on(*args)
+
+        def hand_on(c):
+            cols = slice(c * half, (c + 1) * half)
+            out_word = sb(f"out_word{c}", [P, half], U32)
+            nc.vector.quantize_mx(
+                out=out_word[:].bitcast(FP8X4), scales=out_scale[:, cols], in_=out_bf[c][:].rearrange("p v t -> p (v t)")
+            )
+            nc.sync.dma_start(out=out_words[:, cols], in_=out_word[:].bitcast(I32))
+
+        weigh(3, 0, 0, half)
+        weigh(3, 1, 0, half)
+        weigh(3, 0, half, V)
+        add_terms(0)
+        weigh(3, 1, half, V)
+        last_product(0, nc.scalar.copy)
+        add_terms(1)
+        last_product(1, nc.vector.tensor_copy)
+        hand_on(0)
+        hand_on(1)
         for q in range(QUADS):
             queue = nc.sync if q % 2 == 0 else nc.scalar
             queue.dma_start(

@@ -33,10 +33,10 @@ def load_scales(queue, tile, scales, row, quads=range(QUADS)):
         )
 
 
-def deal(nc, dealt, raw):
+def deal(nc, dealt, raw, line):
     nc.vector.tensor_copy(
-        out=dealt[:].rearrange("p (t c i) -> p c t i", t=PACK, i=4),
-        in_=raw[:].rearrange("p (c i t) -> p c t i", t=PACK, i=4),
+        out=dealt[:].rearrange("p (t c i) -> p c t i", t=PACK, i=line),
+        in_=raw[:].rearrange("p (c i t) -> p c t i", t=PACK, i=line),
     )
 
 
@@ -48,7 +48,8 @@ def tile_picked_zdin_sigmoid_po_kernel(
     with ExitStack() as ctx:
         lists = ctx.enter_context(tc.tile_pool(name="lists", bufs=1))
         keep = ctx.enter_context(tc.tile_pool(name="keep", bufs=1))
-        psum = ctx.enter_context(tc.psum_pool(name="psum", bufs=2))
+        reuse = ctx.enter_context(tc.tile_pool(name="reuse", bufs=1))
+        psum = ctx.enter_context(tc.psum_pool(name="psum", bufs=1))
 
         offs_sb = lists.tile([P, S // 16], U16, name="offs_sb")
         tgt_sb = lists.tile([P, V // 16], U16, name="tgt_sb")
@@ -62,34 +63,42 @@ def tile_picked_zdin_sigmoid_po_kernel(
         w1_raw = sb("w1_raw", [P, N], U32)
         w2_raw = sb("w2_raw", [P, N], U32)
         w4_raw = sb("w4_raw", [P, N], U32)
-        w12_scale_raw = sb("w12_scale_raw", [P, N], U8)
+        w1_scale_raw = sb("w1_scale_raw", [P, N], U8, "w1_then_w3_scale")
+        w2_scale_raw = sb("w2_scale_raw", [P, N], U8)
         w4_scale_raw = sb("w4_scale_raw", [P, N], U8)
-        w3_raw = [sb(f"w3_raw{u}", [P, PACK, H // 2], F32) for u in range(2)]
+        w3_raw = [
+            sb("w3_raw0", [P, PACK, H // 2], F32),
+            reuse.tile([P, PACK, H // 2], F32, name="w3_raw1", offset=0),
+        ]
         warm = sb("warm", [P, 8], F32)
         warm_out = sb("warm_out", [P, 8], F32)
 
-        nc.gpsimd.memset(x_scale[:].bitcast(I32), 0)
-        nc.gpsimd.memset(warm[:], 0.0)
-        nc.vector.memset(w12_scale_raw[:].bitcast(I32), 0)
+        nc.gpsimd.memset(w1_scale_raw[:].bitcast(I32), 0)
+        load_scales(nc.gpsimd, w1_scale_raw, w1_scales, 0, range(3))
+        nc.vector.memset(w2_scale_raw[:].bitcast(I32), 0)
         nc.vector.memset(w4_scale_raw[:].bitcast(I32), 0)
+        nc.vector.memset(warm[:], 0.0)
 
-        nc.sync.dma_start(tgt_sb[:], tgt)
-        load_scales(nc.sync, x_scale, x_scales, 0, range(2))
-        load_scales(nc.scalar, x_scale, x_scales, 0, range(2, 4))
+        w3_rows = w3.rearrange("(p j) c -> p j c", j=PACK)
+        for q in range(QUADS):
+            queue = nc.sync if q < 2 else nc.scalar
+            queue.dma_start(
+                out=x_scale[32 * q : 32 * (q + 1), :].bitcast(I32),
+                in_=x_scales[0, 4 * q : 4 * q + 4, :].bitcast(I32).unsqueeze(0).broadcast_to([8, 4, T // 4]),
+            )
         nc.scalar.activation(out=warm_out[:], in_=warm[:], func=SIGMOID)
         nc.sync.dma_start(offs_sb[:], offs)
+        nc.sync.dma_start(tgt_sb[:], tgt)
         load_words(nc.sync, x_word, x_words)
-        load_words(nc.sync, w1_raw, w1_words)
-        load_words(nc.sync, w2_raw, w2_words)
-        w3_rows = w3.rearrange("(p j) c -> p j c", j=PACK)
         nc.sync.dma_start(out=w3_raw[0][:], in_=w3_rows[:, :, : H // 2])
-        load_scales(nc.sync, w12_scale_raw, w1_scales, 0)
-        load_scales(nc.sync, w12_scale_raw, w2_scales, 4, range(2))
-        load_scales(nc.gpsimd, w12_scale_raw, w2_scales, 4, range(2, 4))
+        load_words(nc.sync, w2_raw, w2_words)
+        load_scales(nc.sync, w2_scale_raw, w2_scales, 0)
         nc.sync.dma_start(out=w3_raw[1][:], in_=w3_rows[:, :, H // 2 :])
+        load_words(nc.sync, w1_raw, w1_words)
+        load_scales(nc.sync, w1_scale_raw, w1_scales, 0, range(3, 4))
+        load_words(nc.sync, w4_raw, w4_words)
         nc.sync.dma_start(pos_sb[0][:], pos1)
         nc.sync.dma_start(pos_sb[1][:], pos2)
-        load_words(nc.sync, w4_raw, w4_words)
         load_scales(nc.sync, w4_scale_raw, w4_scales, 0)
 
         tgt_word = sb("tgt_word", [P, V], U32)
@@ -99,16 +108,18 @@ def tile_picked_zdin_sigmoid_po_kernel(
         w1_word = sb("w1_word", [P, N], U32)
         w2_word = sb("w2_word", [P, N], U32)
         w4_word = sb("w4_word", [P, N], U32)
-        w12_scale = sb("w12_scale", [P, N], U8)
+        w1_scale = sb("w1_scale", [P, N], U8)
+        w2_scale = sb("w2_scale", [P, N], U8)
         w4_scale = sb("w4_scale", [P, N], U8)
 
-        nc.vector.tensor_copy(out=tgt_scale[:], in_=x_scale[:].indirect(tgt_sb[:]))
         nc.vector.tensor_copy(out=hist_scale[:], in_=x_scale[:].indirect(offs_sb[:]))
-        nc.vector.tensor_copy(out=tgt_word[:], in_=x_word[:].indirect(tgt_sb[:]))
-        deal(nc, w1_word, w1_raw)
-        deal(nc, w2_word, w2_raw)
-        deal(nc, w12_scale, w12_scale_raw)
+        nc.vector.tensor_copy(out=tgt_scale[:], in_=x_scale[:].indirect(tgt_sb[:]))
         nc.vector.tensor_copy(out=hist_word[:], in_=x_word[:].indirect(offs_sb[:]))
+        nc.vector.tensor_copy(out=tgt_word[:], in_=x_word[:].indirect(tgt_sb[:]))
+        deal(nc, w2_word, w2_raw, 4)
+        deal(nc, w2_scale, w2_scale_raw, 16)
+        deal(nc, w1_word, w1_raw, 4)
+        deal(nc, w1_scale, w1_scale_raw, 16)
 
         def product(acc, word, scale, row, t, rhs_word, rhs_scale):
             cols = slice(P * t, P * (t + 1))
@@ -119,13 +130,15 @@ def tile_picked_zdin_sigmoid_po_kernel(
 
         y_sb = [sb(f"y_sb{t}", [P, V], F32) for t in range(PACK)]
         e_sb = {}
-        h_sb = [sb(f"h_sb{t}", [P, S], F32) for t in range(PACK)]
+        h_sb = {}
         logit = {}
         gate = [sb(f"gate{t}", [P, 2, V], F32) for t in range(PACK)]
-        term = [sb(f"term{d}", [P, PACK, V], F32) for d in range(2)]
+        terms = sb("terms", [P, 2, PACK, V], F32)
+        term = [terms[:, d] for d in range(2)]
+        half = V // 2
         w3_bf = sb("w3_bf", [P, PACK, P, PACK], BF16)
         w3_word = sb("w3_word", [P, H], U32)
-        w3_scale = sb("w3_scale", [P, H], U8)
+        w3_scale = sb("w3_scale", [P, H], U8, "w1_then_w3_scale")
 
         def round_w3(u, copy):
             copy(
@@ -133,18 +146,21 @@ def tile_picked_zdin_sigmoid_po_kernel(
                 in_=w3_raw[u][:].rearrange("p j (m t) -> p m t j", t=PACK),
             )
 
+        def bank(number, shape):
+            return psum.tile(shape, F32, name="acc", tag=f"bank{number}")
+
         def targets(t):
-            acc = psum.tile([P, V], F32, name="y_ps")
-            product(acc[:], w1_word, w12_scale, 0, t, tgt_word[:], tgt_scale[:])
+            acc = bank((t + 1) % PACK, [P, V])
+            product(acc[:], w1_word, w1_scale, 0, t, tgt_word[:], tgt_scale[:])
             nc.scalar.copy(out=y_sb[t][:], in_=acc[:])
 
-        def history(result, word, scale, row, t, lo=0, hi=S, copy=nc.scalar.copy):
-            acc = psum.tile([P, hi - lo], F32, name="hist_ps", bufs=4)
-            product(acc[:], word, scale, row, t, hist_word[:, lo:hi], hist_scale[:, lo:hi])
-            copy(out=result[t][:, lo:hi], in_=acc[:])
+        def history(result, word, scale, t, number):
+            acc = bank(number, [P, S])
+            product(acc[:], word, scale, 0, t, hist_word[:], hist_scale[:])
+            nc.scalar.copy(out=result[t][:], in_=acc[:])
 
-        def logits(t, tag=""):
-            logit[t] = sb(f"logit{t}", [P, 2, V], F32, tag)
+        def logits(t):
+            logit[t] = sb(f"logit{t}", [P, 2, V], F32, f"logit_then_h{t}")
             for d in range(2):
                 nc.vector.tensor_tensor(
                     out=logit[t][:, d, :], in0=e_sb[t][:].indirect(pos_sb[d][:]), in1=y_sb[t][:], op=MULT
@@ -159,29 +175,28 @@ def tile_picked_zdin_sigmoid_po_kernel(
                 in1=gate[t][:, d, lo:hi], op=MULT,
             )
 
-        def keys(t, tag=""):
-            e_sb[t] = sb(f"e_sb{t}", [P, S], F32, tag)
-            history(e_sb, w2_word, w12_scale, 4, t)
+        def keys(t):
+            if t == 0:
+                e_sb[t] = reuse.tile([P, S], F32, name=f"e_sb{t}", offset=4 * S * t)
+            else:
+                e_sb[t] = sb(f"e_sb{t}", [P, S], F32)
+            history(e_sb, w2_word, w2_scale, t, t)
             targets(t)
 
         round_w3(0, nc.scalar.copy)
-        e_sb[0] = sb("e_sb0", [P, S], F32)
-        history(e_sb, w2_word, w12_scale, 4, 0, 0, S // 2)
-        history(e_sb, w2_word, w12_scale, 4, 0, S // 2, S, nc.vector.tensor_copy)
-        targets(0)
-        round_w3(1, nc.vector.tensor_copy)
+        round_w3(1, nc.scalar.copy)
         nc.vector.quantize_mx(
             out=w3_word[:].bitcast(FP8X4), scales=w3_scale[:], in_=w3_bf[:].rearrange("p t m j -> p (t m j)")
         )
-        logits(0)
-        for t in range(1, PACK):
+        deal(nc, w4_word, w4_raw, 4)
+        for t in range(PACK):
             keys(t)
             logits(t)
-        deal(nc, w4_word, w4_raw)
-        deal(nc, w4_scale, w4_scale_raw)
+        deal(nc, w4_scale, w4_scale_raw, 16)
         for t in range(PACK):
+            h_sb[t] = sb(f"h_sb{t}", [P, S], F32, f"logit_then_h{t - 1}")
+            history(h_sb, w3_word, w3_scale, t, PACK + t)
             gates(t)
-            history(h_sb, w3_word, w3_scale, 0, t)
         for t in range(PACK - 1):
             for d in range(2):
                 weigh(t, d, 0, V)
@@ -189,42 +204,44 @@ def tile_picked_zdin_sigmoid_po_kernel(
         out_rows = out_0.rearrange("(p t) v -> p t v", t=PACK)
         out_words = out_1[0].rearrange("p v t -> p (v t)").bitcast(I32)
         out_scale = sb("out_scale", [P, V], U8)
-        half = V // 2
-        z_bf = [sb(f"z_bf{c}", [P, half, PACK], BF16) for c in range(2)]
-        out_bf = [sb(f"out_bf{c}", [P, half, PACK], BF16) for c in range(2)]
+        z_bf = [sb(f"z_bf{u}", [P, half, PACK], BF16) for u in range(2)]
+        z_word = [sb(f"z_word{u}", [P, half], U32) for u in range(2)]
+        z_scale = [sb(f"z_scale{u}", [P, half], U8) for u in range(2)]
+        out_sb = [sb(f"out_sb{u}", [P, PACK, half], F32) for u in range(2)]
+        out_bf = [sb(f"out_bf{u}", [P, half, PACK], BF16) for u in range(2)]
 
-        def add_terms(c):
-            cols = slice(c * half, (c + 1) * half)
+        def add_terms(u):
+            cols = slice(u * half, (u + 1) * half)
             nc.vector.tensor_tensor(
-                out=z_bf[c][:].rearrange("p (c i) t -> p c t i", i=2),
+                out=z_bf[u][:].rearrange("p (c i) t -> p c t i", i=2),
                 in0=term[0][:, :, cols].rearrange("p t (c i) -> p c t i", i=2),
                 in1=term[1][:, :, cols].rearrange("p t (c i) -> p c t i", i=2),
                 op=ADD,
             )
 
-        def last_product(c, copy):
-            z_word = sb(f"z_word{c}", [P, half], U32)
-            z_scale = sb(f"z_scale{c}", [P, half], U8)
+        def last_product(u, copies):
             nc.vector.quantize_mx(
-                out=z_word[:].bitcast(FP8X4), scales=z_scale[:], in_=z_bf[c][:].rearrange("p v t -> p (v t)")
+                out=z_word[u][:].bitcast(FP8X4), scales=z_scale[u][:], in_=z_bf[u][:].rearrange("p v t -> p (v t)")
             )
-            out_sb = sb(f"out_sb{c}", [P, PACK, half], F32)
-            for u, empty in enumerate((nc.scalar.copy, copy)):
-                out_ps = psum.tile([P, 2, half], F32, name="out_ps")
-                for s in range(2):
-                    product(out_ps[:, s, :], w4_word, w4_scale, 0, 2 * u + s, z_word[:], z_scale[:])
-                empty(out=out_sb[:, 2 * u : 2 * u + 2, :], in_=out_ps[:])
-            nc.sync.dma_start(out=out_rows[:, :, c * half : (c + 1) * half], in_=out_sb[:])
+            tiles = PACK // len(copies)
+            for n, copy in enumerate(copies):
+                acc = bank(u + n, [P, tiles, half])
+                for s in range(tiles):
+                    product(acc[:, s, :], w4_word, w4_scale, 0, tiles * n + s, z_word[u][:], z_scale[u][:])
+                copy(out=out_sb[u][:, tiles * n : tiles * (n + 1), :], in_=acc[:])
+            nc.sync.dma_start(out=out_rows[:, :, u * half : (u + 1) * half], in_=out_sb[u][:])
+
+        def round_result(u, copy):
             copy(
-                out=out_bf[c][:].rearrange("p (c i) t -> p c t i", i=2),
-                in_=out_sb[:].rearrange("p t (c i) -> p c t i", i=2),
+                out=out_bf[u][:].rearrange("p (c i) t -> p c t i", i=2),
+                in_=out_sb[u][:].rearrange("p t (c i) -> p c t i", i=2),
             )
 
-        def hand_on(c):
-            cols = slice(c * half, (c + 1) * half)
-            out_word = sb(f"out_word{c}", [P, half], U32)
+        def hand_on(u):
+            cols = slice(u * half, (u + 1) * half)
+            out_word = sb(f"out_word{u}", [P, half], U32)
             nc.vector.quantize_mx(
-                out=out_word[:].bitcast(FP8X4), scales=out_scale[:, cols], in_=out_bf[c][:].rearrange("p v t -> p (v t)")
+                out=out_word[:].bitcast(FP8X4), scales=out_scale[:, cols], in_=out_bf[u][:].rearrange("p v t -> p (v t)")
             )
             nc.sync.dma_start(out=out_words[:, cols], in_=out_word[:].bitcast(I32))
 
@@ -233,10 +250,12 @@ def tile_picked_zdin_sigmoid_po_kernel(
         weigh(3, 0, half, V)
         add_terms(0)
         weigh(3, 1, half, V)
-        last_product(0, nc.scalar.copy)
+        last_product(0, [nc.scalar.copy])
         add_terms(1)
-        last_product(1, nc.vector.tensor_copy)
+        last_product(1, [nc.scalar.copy, nc.vector.tensor_copy])
+        round_result(0, nc.vector.tensor_copy)
         hand_on(0)
+        round_result(1, nc.vector.tensor_copy)
         hand_on(1)
         for q in range(QUADS):
             queue = nc.sync if q % 2 == 0 else nc.scalar

@@ -1,6 +1,7 @@
 from contextlib import ExitStack
 
 import concourse.mybir as mybir
+from concourse.masks import make_identity
 
 K, T, S, V, H, N = 512, 1024, 512, 256, 512, 512
 FLOPS = 2 * K * (N * V + N * S + H * S) + 2 * H * N * V
@@ -13,22 +14,23 @@ U16 = mybir.dt.uint16
 U8 = mybir.dt.uint8
 FP8X4 = mybir.dt.float8_e4m3fn_x4
 MULT = mybir.AluOpType.mult
-ADD = mybir.AluOpType.add
 SIGMOID = mybir.ActivationFunctionType.Sigmoid
 
 P = 128
 PACK = 4
 QUADS = 4
+TILES = 4
+HALF = V // 2
 
 
 def load_words(queue, tile, words):
     queue.dma_start(out=tile[:].bitcast(I32), in_=words[0].rearrange("p n t -> p (n t)").bitcast(I32))
 
 
-def load_scales(queue, tile, scales, row, quads=range(QUADS)):
+def load_scales(queue, tile, scales, row, column, quads=range(QUADS)):
     for q in quads:
         queue.dma_start(
-            out=tile[32 * q + row : 32 * q + row + 4, :].bitcast(I32),
+            out=tile[32 * q + row : 32 * q + row + 4, column : column + N].bitcast(I32),
             in_=scales[0, 4 * q : 4 * q + 4, :].bitcast(I32),
         )
 
@@ -40,6 +42,13 @@ def deal(nc, dealt, raw, line):
     )
 
 
+def interleave(copy, packed, rows):
+    copy(
+        out=packed.rearrange("p (c i) j -> p c j i", i=4),
+        in_=rows.rearrange("p j (c i) -> p c j i", i=4),
+    )
+
+
 def tile_picked_zdin_sigmoid_po_kernel(
     tc, x_words, x_scales, w1_words, w1_scales, w2_words, w2_scales, w3, w4_words, w4_scales,
     offs, tgt, pos1, pos2, out_0, out_1, out_2,
@@ -48,7 +57,6 @@ def tile_picked_zdin_sigmoid_po_kernel(
     with ExitStack() as ctx:
         lists = ctx.enter_context(tc.tile_pool(name="lists", bufs=1))
         keep = ctx.enter_context(tc.tile_pool(name="keep", bufs=1))
-        reuse = ctx.enter_context(tc.tile_pool(name="reuse", bufs=1))
         psum = ctx.enter_context(tc.psum_pool(name="psum", bufs=1))
 
         offs_sb = lists.tile([P, S // 16], U16, name="offs_sb")
@@ -58,24 +66,24 @@ def tile_picked_zdin_sigmoid_po_kernel(
         def sb(name, shape, dtype, tag=""):
             return keep.tile(shape, dtype, name=name, tag=tag, align_bytes=64)
 
+        def bank(number, shape):
+            return psum.tile(shape, F32, name="acc", tag=f"bank{number}")
+
         x_word = sb("x_word", [P, T], U32)
         x_scale = sb("x_scale", [P, T], U8)
-        w1_raw = sb("w1_raw", [P, N], U32)
-        w2_raw = sb("w2_raw", [P, N], U32)
+        w1_word = sb("w1_word", [P, N], U32)
+        w2_word = sb("w2_word", [P, N], U32)
         w4_raw = sb("w4_raw", [P, N], U32)
-        w1_scale_raw = sb("w1_scale_raw", [P, N], U8, "w1_then_w3_scale")
-        w2_scale_raw = sb("w2_scale_raw", [P, N], U8)
+        w12_scale = sb("w12_scale", [P, N + P], U8)
         w4_scale_raw = sb("w4_scale_raw", [P, N], U8)
-        w3_raw = [
-            sb("w3_raw0", [P, PACK, H // 2], F32),
-            reuse.tile([P, PACK, H // 2], F32, name="w3_raw1", offset=0),
-        ]
+        w3_raw = [sb(f"w3_raw{u}", [P, PACK, H // 2], F32) for u in range(2)]
         warm = sb("warm", [P, 8], F32)
         warm_out = sb("warm_out", [P, 8], F32)
+        identity = sb("identity", [P, P], F32)
 
-        nc.gpsimd.memset(w1_scale_raw[:].bitcast(I32), 0)
-        load_scales(nc.gpsimd, w1_scale_raw, w1_scales, 0, range(3))
-        nc.vector.memset(w2_scale_raw[:].bitcast(I32), 0)
+        nc.gpsimd.memset(w12_scale[:].bitcast(I32), 0)
+        load_scales(nc.gpsimd, w12_scale, w1_scales, 0, P, range(2))
+        make_identity(nc, identity[:])
         nc.vector.memset(w4_scale_raw[:].bitcast(I32), 0)
         nc.vector.memset(warm[:], 0.0)
 
@@ -88,76 +96,60 @@ def tile_picked_zdin_sigmoid_po_kernel(
             )
         nc.scalar.activation(out=warm_out[:], in_=warm[:], func=SIGMOID)
         nc.sync.dma_start(offs_sb[:], offs)
-        nc.sync.dma_start(tgt_sb[:], tgt)
         load_words(nc.sync, x_word, x_words)
+        nc.sync.dma_start(tgt_sb[:], tgt)
+        load_words(nc.sync, w2_word, w2_words)
+        load_scales(nc.sync, w12_scale, w2_scales, 4, 0)
         nc.sync.dma_start(out=w3_raw[0][:], in_=w3_rows[:, :, : H // 2])
-        load_words(nc.sync, w2_raw, w2_words)
-        load_scales(nc.sync, w2_scale_raw, w2_scales, 0)
-        nc.sync.dma_start(out=w3_raw[1][:], in_=w3_rows[:, :, H // 2 :])
-        load_words(nc.sync, w1_raw, w1_words)
-        load_scales(nc.sync, w1_scale_raw, w1_scales, 0, range(3, 4))
-        load_words(nc.sync, w4_raw, w4_words)
+        load_words(nc.sync, w1_word, w1_words)
+        load_scales(nc.sync, w12_scale, w1_scales, 0, P, range(2, 4))
         nc.sync.dma_start(pos_sb[0][:], pos1)
         nc.sync.dma_start(pos_sb[1][:], pos2)
-        load_scales(nc.sync, w4_scale_raw, w4_scales, 0)
+        nc.sync.dma_start(out=w3_raw[1][:], in_=w3_rows[:, :, H // 2 :])
+        load_words(nc.sync, w4_raw, w4_words)
+        load_scales(nc.sync, w4_scale_raw, w4_scales, 0, 0)
 
         tgt_word = sb("tgt_word", [P, V], U32)
         tgt_scale = sb("tgt_scale", [P, V], U8)
         hist_word = sb("hist_word", [P, S], U32)
         hist_scale = sb("hist_scale", [P, S], U8)
-        w1_word = sb("w1_word", [P, N], U32)
-        w2_word = sb("w2_word", [P, N], U32)
-        w4_word = sb("w4_word", [P, N], U32)
-        w1_scale = sb("w1_scale", [P, N], U8)
-        w2_scale = sb("w2_scale", [P, N], U8)
-        w4_scale = sb("w4_scale", [P, N], U8)
-
         nc.vector.tensor_copy(out=hist_scale[:], in_=x_scale[:].indirect(offs_sb[:]))
-        nc.vector.tensor_copy(out=tgt_scale[:], in_=x_scale[:].indirect(tgt_sb[:]))
         nc.vector.tensor_copy(out=hist_word[:], in_=x_word[:].indirect(offs_sb[:]))
+        nc.vector.tensor_copy(out=tgt_scale[:], in_=x_scale[:].indirect(tgt_sb[:]))
         nc.vector.tensor_copy(out=tgt_word[:], in_=x_word[:].indirect(tgt_sb[:]))
-        deal(nc, w2_word, w2_raw, 4)
-        deal(nc, w2_scale, w2_scale_raw, 16)
-        deal(nc, w1_word, w1_raw, 4)
-        deal(nc, w1_scale, w1_scale_raw, 16)
 
-        def product(acc, word, scale, row, t, rhs_word, rhs_scale):
-            cols = slice(P * t, P * (t + 1))
+        def product(acc, word, scale, rhs_word, rhs_scale):
             nc.tensor.matmul_mx(
-                out=acc, lhsT=word[:, cols].bitcast(FP8X4), lhsT_scale=scale[row:P, cols],
+                out=acc, lhsT=word.bitcast(FP8X4), lhsT_scale=scale,
                 rhs=rhs_word.bitcast(FP8X4), rhs_scale=rhs_scale, start=True, stop=True,
             )
 
-        y_sb = [sb(f"y_sb{t}", [P, V], F32) for t in range(PACK)]
-        e_sb = {}
+        def block(t, shift=0):
+            return slice(P * t + shift, P * (t + 1) + shift)
+
+        y_sb = [sb(f"y_sb{t}", [P, V], F32) for t in range(TILES)]
+        e_sb = [sb(f"e_sb{t}", [P, S], F32) for t in range(TILES)]
         h_sb = {}
         logit = {}
-        gate = [sb(f"gate{t}", [P, 2, V], F32) for t in range(PACK)]
-        terms = sb("terms", [P, 2, PACK, V], F32)
-        term = [terms[:, d] for d in range(2)]
-        half = V // 2
-        w3_bf = sb("w3_bf", [P, PACK, P, PACK], BF16)
-        w3_word = sb("w3_word", [P, H], U32)
-        w3_scale = sb("w3_scale", [P, H], U8, "w1_then_w3_scale")
+        gate = [sb(f"gate{t}", [P, 2, V], F32, f"gate_slot{t}") for t in range(TILES)]
+        term = [sb(f"term{t}", [P, 2, V], F32) for t in range(TILES)]
+        w3_bf = [sb(f"w3_bf{u}", [P, H // 2, PACK], BF16) for u in range(2)]
+        w3_word = [sb(f"w3_word{u}", [P, H // 2], U32) for u in range(2)]
+        w3_scale = [sb(f"w3_scale{u}", [P, H // 2], U8) for u in range(2)]
 
-        def round_w3(u, copy):
-            copy(
-                out=w3_bf[:, :, 64 * u : 64 * (u + 1), :].rearrange("p t m j -> p m t j"),
-                in_=w3_raw[u][:].rearrange("p j (m t) -> p m t j", t=PACK),
+        def quantise_w3(u, copy):
+            interleave(copy, w3_bf[u][:], w3_raw[u][:])
+            nc.vector.quantize_mx(
+                out=w3_word[u][:].bitcast(FP8X4), scales=w3_scale[u][:], in_=w3_bf[u][:].rearrange("p c j -> p (c j)")
             )
 
-        def bank(number, shape):
-            return psum.tile(shape, F32, name="acc", tag=f"bank{number}")
-
-        def targets(t):
-            acc = bank((t + 1) % PACK, [P, V])
-            product(acc[:], w1_word, w1_scale, 0, t, tgt_word[:], tgt_scale[:])
+        def keys_and_targets(t):
+            acc = bank(t, [P, S])
+            product(acc[:], w2_word[:, block(t)], w12_scale[4:P, block(t)], hist_word[:], hist_scale[:])
+            nc.scalar.copy(out=e_sb[t][:], in_=acc[:])
+            acc = bank(TILES + t, [P, V])
+            product(acc[:], w1_word[:, block(t)], w12_scale[:, block(t, P)], tgt_word[:], tgt_scale[:])
             nc.scalar.copy(out=y_sb[t][:], in_=acc[:])
-
-        def history(result, word, scale, t, number):
-            acc = bank(number, [P, S])
-            product(acc[:], word, scale, 0, t, hist_word[:], hist_scale[:])
-            nc.scalar.copy(out=result[t][:], in_=acc[:])
 
         def logits(t):
             logit[t] = sb(f"logit{t}", [P, 2, V], F32, f"logit_then_h{t}")
@@ -166,96 +158,99 @@ def tile_picked_zdin_sigmoid_po_kernel(
                     out=logit[t][:, d, :], in0=e_sb[t][:].indirect(pos_sb[d][:]), in1=y_sb[t][:], op=MULT
                 )
 
-        def gates(t):
-            nc.scalar.activation(out=gate[t][:], in_=logit[t][:], func=SIGMOID)
+        def values(t):
+            h_sb[t] = sb(f"h_sb{t}", [P, S], F32, f"logit_then_h{t - 1}")
+            acc = bank(t if t > 0 else 2 * TILES - 1, [P, S])
+            u, cols = t // 2, block(t % 2)
+            product(acc[:], w3_word[u][:, cols], w3_scale[u][:, cols], hist_word[:], hist_scale[:])
+            nc.scalar.copy(out=h_sb[t][:], in_=acc[:])
 
         def weigh(t, d, lo, hi):
             nc.vector.tensor_tensor(
-                out=term[d][:, t, lo:hi], in0=h_sb[t][:].indirect(pos_sb[d][:, lo // 16 : hi // 16]),
+                out=term[t][:, d, lo:hi], in0=h_sb[t][:].indirect(pos_sb[d][:, lo // 16 : hi // 16]),
                 in1=gate[t][:, d, lo:hi], op=MULT,
             )
 
-        def keys(t):
-            if t == 0:
-                e_sb[t] = reuse.tile([P, S], F32, name=f"e_sb{t}", offset=4 * S * t)
-            else:
-                e_sb[t] = sb(f"e_sb{t}", [P, S], F32)
-            history(e_sb, w2_word, w2_scale, t, t)
-            targets(t)
+        def add_turned(acc, t, d, u):
+            nc.tensor.matmul(
+                acc, term[t][:, d, block(u)], identity[:], start=(d == 0), stop=(d == 1), is_transpose=True
+            )
 
-        round_w3(0, nc.scalar.copy)
-        round_w3(1, nc.scalar.copy)
-        nc.vector.quantize_mx(
-            out=w3_word[:].bitcast(FP8X4), scales=w3_scale[:], in_=w3_bf[:].rearrange("p t m j -> p (t m j)")
-        )
-        deal(nc, w4_word, w4_raw, 4)
-        for t in range(PACK):
-            keys(t)
+        quantise_w3(0, nc.vector.tensor_copy)
+        for t in range(TILES):
+            keys_and_targets(t)
             logits(t)
-        deal(nc, w4_scale, w4_scale_raw, 16)
-        for t in range(PACK):
-            h_sb[t] = sb(f"h_sb{t}", [P, S], F32, f"logit_then_h{t - 1}")
-            history(h_sb, w3_word, w3_scale, t, PACK + t)
-            gates(t)
-        for t in range(PACK - 1):
+        quantise_w3(1, nc.scalar.copy)
+        for t in range(TILES):
+            values(t)
+            nc.scalar.activation(out=gate[t][:], in_=logit[t][:], func=SIGMOID)
+
+        last = TILES - 1
+        zt_bf = [sb(f"zt_bf{u}", [P, H], BF16) for u in range(2)]
+        early = [bank(4 * u, [P, last, P]) for u in range(2)]
+        for t in range(last):
             for d in range(2):
                 weigh(t, d, 0, V)
+                for u in range(2):
+                    add_turned(early[u][:, t, :], t, d, u)
+        for u in range(2):
+            nc.scalar.copy(out=zt_bf[u][:, : last * P], in_=early[u][:].rearrange("p t i -> p (t i)"))
 
         out_rows = out_0.rearrange("(p t) v -> p t v", t=PACK)
         out_words = out_1[0].rearrange("p v t -> p (v t)").bitcast(I32)
         out_scale = sb("out_scale", [P, V], U8)
-        z_bf = [sb(f"z_bf{u}", [P, half, PACK], BF16) for u in range(2)]
-        z_word = [sb(f"z_word{u}", [P, half], U32) for u in range(2)]
-        z_scale = [sb(f"z_scale{u}", [P, half], U8) for u in range(2)]
-        out_sb = [sb(f"out_sb{u}", [P, PACK, half], F32) for u in range(2)]
-        out_bf = [sb(f"out_bf{u}", [P, half, PACK], BF16) for u in range(2)]
+        z_bf = [sb(f"z_bf{u}", [P, HALF, PACK], BF16) for u in range(2)]
+        z_word = [sb(f"z_word{u}", [P, HALF], U32) for u in range(2)]
+        z_scale = [sb(f"z_scale{u}", [P, HALF], U8) for u in range(2)]
+        out_sb = [sb(f"out_sb{u}", [P, PACK, HALF], F32) for u in range(2)]
+        out_bf = [sb(f"out_bf{u}", [P, HALF, PACK], BF16) for u in range(2)]
 
-        def add_terms(u):
-            cols = slice(u * half, (u + 1) * half)
-            nc.vector.tensor_tensor(
-                out=z_bf[u][:].rearrange("p (c i) t -> p c t i", i=2),
-                in0=term[0][:, :, cols].rearrange("p t (c i) -> p c t i", i=2),
-                in1=term[1][:, :, cols].rearrange("p t (c i) -> p c t i", i=2),
-                op=ADD,
+        def finish_z(u):
+            late = bank(5 + u, [P, P])
+            for d in range(2):
+                weigh(last, d, u * HALF, (u + 1) * HALF)
+                add_turned(late[:], last, d, u)
+            nc.scalar.copy(out=zt_bf[u][:, last * P :], in_=late[:])
+            back = bank(7 if u == 0 else 1, [P, 2, HALF])
+            pairs = zt_bf[u][:].bitcast(F32)
+            for k in range(2):
+                nc.tensor.transpose(back[:, k, :], pairs[:, k : H // 2 : 2], identity[:])
+            return back
+
+        def last_product(u, back, banks, copies):
+            nc.scalar.copy(
+                out=z_bf[u][:].rearrange("p v t -> p (v t)").bitcast(F32).rearrange("p (v k) -> p v k", k=2),
+                in_=back[:].rearrange("p k v -> p v k"),
             )
-
-        def last_product(u, copies):
             nc.vector.quantize_mx(
                 out=z_word[u][:].bitcast(FP8X4), scales=z_scale[u][:], in_=z_bf[u][:].rearrange("p v t -> p (v t)")
             )
             tiles = PACK // len(copies)
             for n, copy in enumerate(copies):
-                acc = bank(u + n, [P, tiles, half])
+                acc = bank(banks[n], [P, tiles, HALF])
                 for s in range(tiles):
-                    product(acc[:, s, :], w4_word, w4_scale, 0, tiles * n + s, z_word[u][:], z_scale[u][:])
+                    cols = block(tiles * n + s)
+                    product(acc[:, s, :], w4_word[:, cols], w4_scale[:, cols], z_word[u][:], z_scale[u][:])
                 copy(out=out_sb[u][:, tiles * n : tiles * (n + 1), :], in_=acc[:])
-            nc.sync.dma_start(out=out_rows[:, :, u * half : (u + 1) * half], in_=out_sb[u][:])
-
-        def round_result(u, copy):
-            copy(
-                out=out_bf[u][:].rearrange("p (c i) t -> p c t i", i=2),
-                in_=out_sb[u][:].rearrange("p t (c i) -> p c t i", i=2),
-            )
+            nc.sync.dma_start(out=out_rows[:, :, block(u)], in_=out_sb[u][:])
 
         def hand_on(u):
-            cols = slice(u * half, (u + 1) * half)
-            out_word = sb(f"out_word{u}", [P, half], U32)
+            interleave(nc.vector.tensor_copy, out_bf[u][:], out_sb[u][:])
+            out_word = sb(f"out_word{u}", [P, HALF], U32)
             nc.vector.quantize_mx(
-                out=out_word[:].bitcast(FP8X4), scales=out_scale[:, cols], in_=out_bf[u][:].rearrange("p v t -> p (v t)")
+                out=out_word[:].bitcast(FP8X4), scales=out_scale[:, block(u)],
+                in_=out_bf[u][:].rearrange("p v t -> p (v t)"),
             )
-            nc.sync.dma_start(out=out_words[:, cols], in_=out_word[:].bitcast(I32))
+            nc.sync.dma_start(out=out_words[:, block(u)], in_=out_word[:].bitcast(I32))
 
-        weigh(3, 0, 0, half)
-        weigh(3, 1, 0, half)
-        weigh(3, 0, half, V)
-        add_terms(0)
-        weigh(3, 1, half, V)
-        last_product(0, [nc.scalar.copy])
-        add_terms(1)
-        last_product(1, [nc.scalar.copy, nc.vector.tensor_copy])
-        round_result(0, nc.vector.tensor_copy)
+        backs = [finish_z(u) for u in range(2)]
+        w4_word = sb("w4_word", [P, N], U32, f"gate_slot{last}")
+        w4_scale = sb("w4_scale", [P, N], U8, f"logit_then_h{last - 1}")
+        deal(nc, w4_word, w4_raw, 4)
+        deal(nc, w4_scale, w4_scale_raw, 16)
+        last_product(0, backs[0], [2], [nc.scalar.copy])
+        last_product(1, backs[1], [3, 0], [nc.scalar.copy, nc.vector.tensor_copy])
         hand_on(0)
-        round_result(1, nc.vector.tensor_copy)
         hand_on(1)
         for q in range(QUADS):
             queue = nc.sync if q % 2 == 0 else nc.scalar

@@ -20,7 +20,14 @@ P = 128
 PACK = 4
 QUADS = 4
 TILES = 4
+LAST = TILES - 1
 HALF = V // 2
+LINE = 16
+W2_ROW = 4
+
+
+def block(n, shift=0):
+    return slice(P * n + shift, P * (n + 1) + shift)
 
 
 def load_words(queue, tile, words):
@@ -35,17 +42,17 @@ def load_scales(queue, tile, scales, row, column, quads=range(QUADS)):
         )
 
 
-def deal(nc, dealt, raw, line):
+def deal(nc, dealt, raw, run):
     nc.vector.tensor_copy(
-        out=dealt[:].rearrange("p (t c i) -> p c t i", t=PACK, i=line),
-        in_=raw[:].rearrange("p (c i t) -> p c t i", t=PACK, i=line),
+        out=dealt[:].rearrange("p (t c i) -> p c t i", t=PACK, i=run),
+        in_=raw[:].rearrange("p (c i t) -> p c t i", t=PACK, i=run),
     )
 
 
 def interleave(copy, packed, rows):
     copy(
-        out=packed.rearrange("p (c i) j -> p c j i", i=4),
-        in_=rows.rearrange("p j (c i) -> p c j i", i=4),
+        out=packed.rearrange("p (c i) j -> p c j i", i=LINE // 4),
+        in_=rows.rearrange("p j (c i) -> p c j i", i=LINE // 4),
     )
 
 
@@ -89,7 +96,7 @@ def tile_picked_zdin_sigmoid_po_kernel(
 
         w3_rows = w3.rearrange("(p j) c -> p j c", j=PACK)
         for q in range(QUADS):
-            queue = nc.sync if q < 2 else nc.scalar
+            queue = nc.sync if q < QUADS // 2 else nc.scalar
             queue.dma_start(
                 out=x_scale[32 * q : 32 * (q + 1), :].bitcast(I32),
                 in_=x_scales[0, 4 * q : 4 * q + 4, :].bitcast(I32).unsqueeze(0).broadcast_to([8, 4, T // 4]),
@@ -99,10 +106,10 @@ def tile_picked_zdin_sigmoid_po_kernel(
         load_words(nc.sync, x_word, x_words)
         nc.sync.dma_start(tgt_sb[:], tgt)
         load_words(nc.sync, w2_word, w2_words)
-        load_scales(nc.sync, w12_scale, w2_scales, 4, 0)
+        load_scales(nc.sync, w12_scale, w2_scales, W2_ROW, 0)
         nc.sync.dma_start(out=w3_raw[0][:], in_=w3_rows[:, :, : H // 2])
         load_words(nc.sync, w1_word, w1_words)
-        load_scales(nc.sync, w12_scale, w1_scales, 0, P, range(2, 4))
+        load_scales(nc.sync, w12_scale, w1_scales, 0, P, range(2, QUADS))
         nc.sync.dma_start(pos_sb[0][:], pos1)
         nc.sync.dma_start(pos_sb[1][:], pos2)
         nc.sync.dma_start(out=w3_raw[1][:], in_=w3_rows[:, :, H // 2 :])
@@ -124,9 +131,6 @@ def tile_picked_zdin_sigmoid_po_kernel(
                 rhs=rhs_word.bitcast(FP8X4), rhs_scale=rhs_scale, start=True, stop=True,
             )
 
-        def block(t, shift=0):
-            return slice(P * t + shift, P * (t + 1) + shift)
-
         y_sb = [sb(f"y_sb{t}", [P, V], F32) for t in range(TILES)]
         e_sb = [sb(f"e_sb{t}", [P, S], F32) for t in range(TILES)]
         h_sb = {}
@@ -145,7 +149,7 @@ def tile_picked_zdin_sigmoid_po_kernel(
 
         def keys_and_targets(t):
             acc = bank(t, [P, S])
-            product(acc[:], w2_word[:, block(t)], w12_scale[4:P, block(t)], hist_word[:], hist_scale[:])
+            product(acc[:], w2_word[:, block(t)], w12_scale[W2_ROW:P, block(t)], hist_word[:], hist_scale[:])
             nc.scalar.copy(out=e_sb[t][:], in_=acc[:])
             acc = bank(TILES + t, [P, V])
             product(acc[:], w1_word[:, block(t)], w12_scale[:, block(t, P)], tgt_word[:], tgt_scale[:])
@@ -160,7 +164,7 @@ def tile_picked_zdin_sigmoid_po_kernel(
 
         def values(t):
             h_sb[t] = sb(f"h_sb{t}", [P, S], F32, f"logit_then_h{t - 1}")
-            acc = bank(t if t > 0 else 2 * TILES - 1, [P, S])
+            acc = bank(t if t > 0 else TILES + LAST, [P, S])
             u, cols = t // 2, block(t % 2)
             product(acc[:], w3_word[u][:, cols], w3_scale[u][:, cols], hist_word[:], hist_scale[:])
             nc.scalar.copy(out=h_sb[t][:], in_=acc[:])
@@ -185,16 +189,22 @@ def tile_picked_zdin_sigmoid_po_kernel(
             values(t)
             nc.scalar.activation(out=gate[t][:], in_=logit[t][:], func=SIGMOID)
 
-        last = TILES - 1
-        zt_bf = [sb(f"zt_bf{u}", [P, H], BF16) for u in range(2)]
-        early = [bank(4 * u, [P, last, P]) for u in range(2)]
-        for t in range(last):
+        zt_bf = [sb(f"zt_bf{u}", [P, 2, P, 2], BF16) for u in range(2)]
+
+        def round_turned(acc, u, first, count):
+            nc.scalar.copy(
+                out=zt_bf[u][:, :, 32 * first : 32 * (first + count), :],
+                in_=acc[:].rearrange("p t (m k e) -> p k (t m) e", k=2, e=2),
+            )
+
+        early = [bank(TILES * u, [P, LAST, P]) for u in range(2)]
+        for t in range(LAST):
             for d in range(2):
                 weigh(t, d, 0, V)
                 for u in range(2):
                     add_turned(early[u][:, t, :], t, d, u)
         for u in range(2):
-            nc.scalar.copy(out=zt_bf[u][:, : last * P], in_=early[u][:].rearrange("p t i -> p (t i)"))
+            round_turned(early[u], u, 0, LAST)
 
         out_rows = out_0.rearrange("(p t) v -> p t v", t=PACK)
         out_words = out_1[0].rearrange("p v t -> p (v t)").bitcast(I32)
@@ -205,16 +215,16 @@ def tile_picked_zdin_sigmoid_po_kernel(
         out_sb = [sb(f"out_sb{u}", [P, PACK, HALF], F32) for u in range(2)]
         out_bf = [sb(f"out_bf{u}", [P, HALF, PACK], BF16) for u in range(2)]
 
-        def finish_z(u):
-            late = bank(5 + u, [P, P])
+        def finish_z(u, sum_bank, back_bank):
+            late = bank(sum_bank, [P, 1, P])
             for d in range(2):
-                weigh(last, d, u * HALF, (u + 1) * HALF)
-                add_turned(late[:], last, d, u)
-            nc.scalar.copy(out=zt_bf[u][:, last * P :], in_=late[:])
-            back = bank(7 if u == 0 else 1, [P, 2, HALF])
-            pairs = zt_bf[u][:].bitcast(F32)
+                weigh(LAST, d, u * HALF, (u + 1) * HALF)
+                add_turned(late[:, 0, :], LAST, d, u)
+            round_turned(late, u, LAST, 1)
+            back = bank(back_bank, [P, 2, HALF])
+            pairs = zt_bf[u][:].rearrange("p k m e -> p (k m e)").bitcast(F32)
             for k in range(2):
-                nc.tensor.transpose(back[:, k, :], pairs[:, k : H // 2 : 2], identity[:])
+                nc.tensor.transpose(back[:, k, :], pairs[:, block(k)], identity[:])
             return back
 
         def last_product(u, back, banks, copies):
@@ -225,13 +235,13 @@ def tile_picked_zdin_sigmoid_po_kernel(
             nc.vector.quantize_mx(
                 out=z_word[u][:].bitcast(FP8X4), scales=z_scale[u][:], in_=z_bf[u][:].rearrange("p v t -> p (v t)")
             )
-            tiles = PACK // len(copies)
+            share = PACK // len(copies)
             for n, copy in enumerate(copies):
-                acc = bank(banks[n], [P, tiles, HALF])
-                for s in range(tiles):
-                    cols = block(tiles * n + s)
+                acc = bank(banks[n], [P, share, HALF])
+                for s in range(share):
+                    cols = block(share * n + s)
                     product(acc[:, s, :], w4_word[:, cols], w4_scale[:, cols], z_word[u][:], z_scale[u][:])
-                copy(out=out_sb[u][:, tiles * n : tiles * (n + 1), :], in_=acc[:])
+                copy(out=out_sb[u][:, share * n : share * (n + 1), :], in_=acc[:])
             nc.sync.dma_start(out=out_rows[:, :, block(u)], in_=out_sb[u][:])
 
         def hand_on(u):
@@ -243,13 +253,13 @@ def tile_picked_zdin_sigmoid_po_kernel(
             )
             nc.sync.dma_start(out=out_words[:, block(u)], in_=out_word[:].bitcast(I32))
 
-        backs = [finish_z(u) for u in range(2)]
-        w4_word = sb("w4_word", [P, N], U32, f"gate_slot{last}")
-        w4_scale = sb("w4_scale", [P, N], U8, f"logit_then_h{last - 1}")
-        deal(nc, w4_word, w4_raw, 4)
-        deal(nc, w4_scale, w4_scale_raw, 16)
+        backs = [finish_z(0, 5, 7), finish_z(1, 6, 1)]
+        w4_word = sb("w4_word", [P, N], U32, f"gate_slot{LAST}")
+        w4_scale = sb("w4_scale", [P, N], U8, f"logit_then_h{LAST - 1}")
+        deal(nc, w4_word, w4_raw, LINE // 4)
+        deal(nc, w4_scale, w4_scale_raw, LINE)
         last_product(0, backs[0], [2], [nc.scalar.copy])
-        last_product(1, backs[1], [3, 0], [nc.scalar.copy, nc.vector.tensor_copy])
+        last_product(1, backs[1], [3, 0], [nc.vector.tensor_copy, nc.scalar.copy])
         hand_on(0)
         hand_on(1)
         for q in range(QUADS):

@@ -1,7 +1,6 @@
 from contextlib import ExitStack
 
 import concourse.mybir as mybir
-from concourse.masks import make_identity
 
 K, T, S, V, H, N = 512, 1024, 512, 256, 512, 512
 FLOPS = 2 * K * (N * V + N * S + H * S) + 2 * H * N * V
@@ -14,7 +13,9 @@ U16 = mybir.dt.uint16
 U8 = mybir.dt.uint8
 FP8X4 = mybir.dt.float8_e4m3fn_x4
 MULT = mybir.AluOpType.mult
+ADD = mybir.AluOpType.add
 SIGMOID = mybir.ActivationFunctionType.Sigmoid
+COPY = mybir.ActivationFunctionType.Copy
 
 P = 128
 PACK = 4
@@ -26,33 +27,30 @@ LINE = 16
 W2_ROW = 4
 
 
-def block(n, shift=0):
-    return slice(P * n + shift, P * (n + 1) + shift)
+def block(n):
+    return slice(P * n, P * (n + 1))
+
+
+def half_of(offsets, u):
+    return offsets[:, u * HALF // 16 : (u + 1) * HALF // 16]
 
 
 def load_words(queue, tile, words):
     queue.dma_start(out=tile[:].bitcast(I32), in_=words[0].rearrange("p n t -> p (n t)").bitcast(I32))
 
 
-def load_scales(queue, tile, scales, row, column, quads=range(QUADS)):
+def load_scales(queue, tile, scales, row, quads=range(QUADS)):
     for q in quads:
         queue.dma_start(
-            out=tile[32 * q + row : 32 * q + row + 4, column : column + N].bitcast(I32),
+            out=tile[32 * q + row : 32 * q + row + 4, :].bitcast(I32),
             in_=scales[0, 4 * q : 4 * q + 4, :].bitcast(I32),
         )
 
 
-def deal(nc, dealt, raw, run):
-    nc.vector.tensor_copy(
+def deal(engine, dealt, raw, run):
+    engine.tensor_copy(
         out=dealt[:].rearrange("p (t c i) -> p c t i", t=PACK, i=run),
         in_=raw[:].rearrange("p (c i t) -> p c t i", t=PACK, i=run),
-    )
-
-
-def interleave(copy, packed, rows):
-    copy(
-        out=packed.rearrange("p (c i) j -> p c j i", i=LINE // 4),
-        in_=rows.rearrange("p j (c i) -> p c j i", i=LINE // 4),
     )
 
 
@@ -64,6 +62,7 @@ def tile_picked_zdin_sigmoid_po_kernel(
     with ExitStack() as ctx:
         lists = ctx.enter_context(tc.tile_pool(name="lists", bufs=1))
         keep = ctx.enter_context(tc.tile_pool(name="keep", bufs=1))
+        reuse = ctx.enter_context(tc.tile_pool(name="reuse", bufs=1))
         psum = ctx.enter_context(tc.psum_pool(name="psum", bufs=1))
 
         offs_sb = lists.tile([P, S // 16], U16, name="offs_sb")
@@ -73,57 +72,71 @@ def tile_picked_zdin_sigmoid_po_kernel(
         def sb(name, shape, dtype, tag=""):
             return keep.tile(shape, dtype, name=name, tag=tag, align_bytes=64)
 
+        def placed(name, shape, dtype, offset):
+            return reuse.tile(shape, dtype, name=name, offset=offset, align_bytes=64)
+
         def bank(number, shape):
             return psum.tile(shape, F32, name="acc", tag=f"bank{number}")
 
         x_word = sb("x_word", [P, T], U32)
         x_scale = sb("x_scale", [P, T], U8)
-        w1_word = sb("w1_word", [P, N], U32)
-        w2_word = sb("w2_word", [P, N], U32)
+        w1_raw = sb("w1_raw", [P, N], U32)
+        w2_raw = sb("w2_raw", [P, N], U32)
         w4_raw = sb("w4_raw", [P, N], U32)
-        w12_scale = sb("w12_scale", [P, N + P], U8)
+        w12_scale_raw = placed("w12_scale_raw", [P, N], U8, 6144 + 448)
         w4_scale_raw = sb("w4_scale_raw", [P, N], U8)
-        w3_raw = [sb(f"w3_raw{u}", [P, PACK, H // 2], F32) for u in range(2)]
+        w3_raw = [
+            sb("w3_raw0", [P, PACK, H // 2], F32),
+            reuse.tile([P, PACK, H // 2], F32, name="w3_raw1", offset=1984, align_bytes=64),
+        ]
         warm = sb("warm", [P, 8], F32)
         warm_out = sb("warm_out", [P, 8], F32)
-        identity = sb("identity", [P, P], F32)
 
-        nc.gpsimd.memset(w12_scale[:].bitcast(I32), 0)
-        load_scales(nc.gpsimd, w12_scale, w1_scales, 0, P, range(2))
-        make_identity(nc, identity[:])
-        nc.vector.memset(w4_scale_raw[:].bitcast(I32), 0)
+        nc.gpsimd.memset(w12_scale_raw[:].bitcast(I32), 0)
+        load_scales(nc.gpsimd, w12_scale_raw, w1_scales, 0, range(LAST))
         nc.vector.memset(warm[:], 0.0)
+        nc.vector.memset(w4_scale_raw[:].bitcast(I32), 0)
 
-        w3_rows = w3.rearrange("(p j) c -> p j c", j=PACK)
-        for q in range(QUADS):
-            queue = nc.sync if q < QUADS // 2 else nc.scalar
+        def load_x_scale(queue, q):
             queue.dma_start(
                 out=x_scale[32 * q : 32 * (q + 1), :].bitcast(I32),
                 in_=x_scales[0, 4 * q : 4 * q + 4, :].bitcast(I32).unsqueeze(0).broadcast_to([8, 4, T // 4]),
             )
+
+        w3_rows = w3.rearrange("(p j) c -> p j c", j=PACK)
+        for q in range(QUADS):
+            load_x_scale(nc.sync if q < QUADS // 2 else nc.scalar, q)
         nc.scalar.activation(out=warm_out[:], in_=warm[:], func=SIGMOID)
         nc.sync.dma_start(offs_sb[:], offs)
         load_words(nc.sync, x_word, x_words)
+        load_words(nc.sync, w2_raw, w2_words)
+        load_words(nc.sync, w1_raw, w1_words)
         nc.sync.dma_start(tgt_sb[:], tgt)
-        load_words(nc.sync, w2_word, w2_words)
-        load_scales(nc.sync, w12_scale, w2_scales, W2_ROW, 0)
+        load_scales(nc.sync, w12_scale_raw, w2_scales, W2_ROW)
+        load_scales(nc.sync, w12_scale_raw, w1_scales, 0, [LAST])
         nc.sync.dma_start(out=w3_raw[0][:], in_=w3_rows[:, :, : H // 2])
-        load_words(nc.sync, w1_word, w1_words)
-        load_scales(nc.sync, w12_scale, w1_scales, 0, P, range(2, QUADS))
         nc.sync.dma_start(pos_sb[0][:], pos1)
         nc.sync.dma_start(pos_sb[1][:], pos2)
         nc.sync.dma_start(out=w3_raw[1][:], in_=w3_rows[:, :, H // 2 :])
         load_words(nc.sync, w4_raw, w4_words)
-        load_scales(nc.sync, w4_scale_raw, w4_scales, 0, 0)
+        load_scales(nc.sync, w4_scale_raw, w4_scales, 0)
 
-        tgt_word = sb("tgt_word", [P, V], U32)
         tgt_scale = sb("tgt_scale", [P, V], U8)
-        hist_word = sb("hist_word", [P, S], U32)
+        hist_word = [sb(f"hist_word{u}", [P, V], U32) for u in range(2)]
         hist_scale = sb("hist_scale", [P, S], U8)
+        w1_word = sb("w1_word", [P, N], U32)
+        w2_word = sb("w2_word", [P, N], U32)
+        w12_scale = sb("w12_scale", [P, N], U8)
         nc.vector.tensor_copy(out=hist_scale[:], in_=x_scale[:].indirect(offs_sb[:]))
-        nc.vector.tensor_copy(out=hist_word[:], in_=x_word[:].indirect(offs_sb[:]))
+        for u in range(2):
+            nc.vector.tensor_copy(out=hist_word[u][:], in_=x_word[:].indirect(offs_sb[:, 16 * u : 16 * (u + 1)]))
+        deal(nc.gpsimd, w2_word, w2_raw, LINE // 4)
+        deal(nc.gpsimd, w1_word, w1_raw, LINE // 4)
         nc.vector.tensor_copy(out=tgt_scale[:], in_=x_scale[:].indirect(tgt_sb[:]))
-        nc.vector.tensor_copy(out=tgt_word[:], in_=x_word[:].indirect(tgt_sb[:]))
+        deal(nc.vector, w12_scale, w12_scale_raw, LINE)
+        tgt_word = [placed(f"tgt_word{u}", [P, HALF], U32, 6144 + 512 * u) for u in range(2)]
+        for u in range(2):
+            nc.vector.tensor_copy(out=tgt_word[u][:], in_=x_word[:].indirect(half_of(tgt_sb, u)))
 
         def product(acc, word, scale, rhs_word, rhs_scale):
             nc.tensor.matmul_mx(
@@ -132,79 +145,95 @@ def tile_picked_zdin_sigmoid_po_kernel(
             )
 
         y_sb = [sb(f"y_sb{t}", [P, V], F32) for t in range(TILES)]
-        e_sb = [sb(f"e_sb{t}", [P, S], F32) for t in range(TILES)]
+        e_sb = [sb(f"e_sb{t}", [P, S], F32) for t in range(2)]
         h_sb = {}
         logit = {}
-        gate = [sb(f"gate{t}", [P, 2, V], F32, f"gate_slot{t}") for t in range(TILES)]
-        term = [sb(f"term{t}", [P, 2, V], F32) for t in range(TILES)]
-        w3_bf = [sb(f"w3_bf{u}", [P, H // 2, PACK], BF16) for u in range(2)]
-        w3_word = [sb(f"w3_word{u}", [P, H // 2], U32) for u in range(2)]
-        w3_scale = [sb(f"w3_scale{u}", [P, H // 2], U8) for u in range(2)]
+        gate = {}
+        term = sb("term", [P, 2, TILES, V], F32)
+        w3_bf = sb("w3_bf", [P, TILES, P, PACK], BF16)
+        w3_word = sb("w3_word", [P, H], U32)
+        w3_scale = sb("w3_scale", [P, H], U8)
 
-        def quantise_w3(u, copy):
-            interleave(copy, w3_bf[u][:], w3_raw[u][:])
-            nc.vector.quantize_mx(
-                out=w3_word[u][:].bitcast(FP8X4), scales=w3_scale[u][:], in_=w3_bf[u][:].rearrange("p c j -> p (c j)")
+        def round_w3(u, copy):
+            copy(
+                out=w3_bf[:, :, 64 * u : 64 * (u + 1), :].rearrange("p t (c i) j -> p c j i t", i=2),
+                in_=w3_raw[u][:].rearrange("p j (c i t) -> p c j i t", i=2, t=PACK),
             )
+
+        def over_history(acc, part, word, scale):
+            for n, u in enumerate(part):
+                product(acc[:, n, :], word, scale, hist_word[u][:], hist_scale[:, u * V : (u + 1) * V])
 
         def keys_and_targets(t):
-            acc = bank(t, [P, S])
-            product(acc[:], w2_word[:, block(t)], w12_scale[W2_ROW:P, block(t)], hist_word[:], hist_scale[:])
-            nc.scalar.copy(out=e_sb[t][:], in_=acc[:])
-            acc = bank(TILES + t, [P, V])
-            product(acc[:], w1_word[:, block(t)], w12_scale[:, block(t, P)], tgt_word[:], tgt_scale[:])
-            nc.scalar.copy(out=y_sb[t][:], in_=acc[:])
-
-        def logits(t):
-            logit[t] = sb(f"logit{t}", [P, 2, V], F32, f"logit_then_h{t}")
-            for d in range(2):
-                nc.vector.tensor_tensor(
-                    out=logit[t][:, d, :], in0=e_sb[t][:].indirect(pos_sb[d][:]), in1=y_sb[t][:], op=MULT
+            parts = [[0], [1]] if t == 0 else [[0, 1]]
+            for part in parts:
+                acc = bank(max(t, part[0]), [P, len(part), V])
+                over_history(acc, part, w2_word[:, block(t)], w12_scale[W2_ROW:P, block(t)])
+                nc.scalar.copy(out=e_sb[t][:, part[0] * V : (part[-1] + 1) * V], in_=acc[:].rearrange("p n v -> p (n v)"))
+            for part in parts:
+                acc = bank(2 + part[0] if t == 0 else LAST + t, [P, len(part), HALF])
+                for n, u in enumerate(part):
+                    product(
+                        acc[:, n, :], w1_word[:, block(t)], w12_scale[:, block(t)], tgt_word[u][:], tgt_scale[:, block(u)]
+                    )
+                nc.scalar.copy(
+                    out=y_sb[t][:, part[0] * HALF : (part[-1] + 1) * HALF], in_=acc[:].rearrange("p n v -> p (n v)")
                 )
 
+        def logits(t):
+            logit[t] = sb(f"logit{t}", [P, 2, V], F32, f"logit_slot{t}")
+            for lo, hi in [(0, HALF), (HALF, V)] if t == 0 else [(0, V)]:
+                for d in range(2):
+                    nc.vector.tensor_tensor(
+                        out=logit[t][:, d, lo:hi], in0=e_sb[t][:].indirect(pos_sb[d][:, lo // 16 : hi // 16]),
+                        in1=y_sb[t][:, lo:hi], op=MULT,
+                    )
+
         def values(t):
-            h_sb[t] = sb(f"h_sb{t}", [P, S], F32, f"logit_then_h{t - 1}")
-            acc = bank(t if t > 0 else TILES + LAST, [P, S])
-            u, cols = t // 2, block(t % 2)
-            product(acc[:], w3_word[u][:, cols], w3_scale[u][:, cols], hist_word[:], hist_scale[:])
-            nc.scalar.copy(out=h_sb[t][:], in_=acc[:])
+            h_sb[t] = sb(f"h_sb{t}", [P, S], F32)
+            acc = bank([6, 0, 7, 4][t], [P, 2, V])
+            over_history(acc, [0, 1], w3_word[:, block(t)], w3_scale[:, block(t)])
+            nc.scalar.copy(out=h_sb[t][:], in_=acc[:].rearrange("p n v -> p (n v)"))
 
-        def weigh(t, d, lo, hi):
+        def weigh(t, d):
             nc.vector.tensor_tensor(
-                out=term[t][:, d, lo:hi], in0=h_sb[t][:].indirect(pos_sb[d][:, lo // 16 : hi // 16]),
-                in1=gate[t][:, d, lo:hi], op=MULT,
+                out=term[:, d, t, :], in0=h_sb[t][:].indirect(pos_sb[d][:]), in1=gate[t][:, d, :], op=MULT,
             )
 
-        def add_turned(acc, t, d, u):
-            nc.tensor.matmul(
-                acc, term[t][:, d, block(u)], identity[:], start=(d == 0), stop=(d == 1), is_transpose=True
-            )
-
-        quantise_w3(0, nc.vector.tensor_copy)
-        for t in range(TILES):
+        round_w3(0, nc.vector.tensor_copy)
+        for t in range(2):
             keys_and_targets(t)
             logits(t)
-        quantise_w3(1, nc.scalar.copy)
+        round_w3(1, nc.scalar.copy)
+        nc.vector.quantize_mx(
+            out=w3_word[:].bitcast(FP8X4), scales=w3_scale[:], in_=w3_bf[:].rearrange("p t m j -> p (t m j)")
+        )
+        e_sb.append(reuse.tile([P, S], F32, name="e_sb2", offset=4096, align_bytes=64))
+        e_sb.append(reuse.tile([P, S], F32, name="e_sb3", offset=0, align_bytes=64))
+        for t in range(2, TILES):
+            keys_and_targets(t)
+            logits(t)
+        w4_word = sb("w4_word", [P, N], U32)
+        w4_scale = sb("w4_scale", [P, N], U8)
+        deal(nc.vector, w4_word, w4_raw, LINE // 4)
+        deal(nc.vector, w4_scale, w4_scale_raw, LINE)
         for t in range(TILES):
             values(t)
+            if t == 0:
+                gate[t] = placed("gate0", [P, 2, V], F32, 2048)
+            else:
+                gate[t] = sb(f"gate{t}", [P, 2, V], F32, "logit_slot0" if t == 1 else "")
             nc.scalar.activation(out=gate[t][:], in_=logit[t][:], func=SIGMOID)
-
-        zt_bf = [sb(f"zt_bf{u}", [P, 2, P, 2], BF16) for u in range(2)]
-
-        def round_turned(acc, u, first, count):
-            nc.scalar.copy(
-                out=zt_bf[u][:, :, 32 * first : 32 * (first + count), :],
-                in_=acc[:].rearrange("p t (m k e) -> p k (t m) e", k=2, e=2),
-            )
-
-        early = [bank(TILES * u, [P, LAST, P]) for u in range(2)]
+        picked = sb("picked", [P, 2, V], F32)
+        for d in range(2):
+            nc.scalar.activation(out=picked[:, d, :], in_=h_sb[LAST][:].indirect(pos_sb[d][:]), func=COPY)
         for t in range(LAST):
             for d in range(2):
-                weigh(t, d, 0, V)
-                for u in range(2):
-                    add_turned(early[u][:, t, :], t, d, u)
+                weigh(t, d)
         for u in range(2):
-            round_turned(early[u], u, 0, LAST)
+            nc.vector.tensor_tensor(
+                out=term[:, :, LAST, block(u)], in0=picked[:, :, block(u)], in1=gate[LAST][:, :, block(u)], op=MULT
+            )
 
         out_rows = out_0.rearrange("(p t) v -> p t v", t=PACK)
         out_words = out_1[0].rearrange("p v t -> p (v t)").bitcast(I32)
@@ -214,24 +243,16 @@ def tile_picked_zdin_sigmoid_po_kernel(
         z_scale = [sb(f"z_scale{u}", [P, HALF], U8) for u in range(2)]
         out_sb = [sb(f"out_sb{u}", [P, PACK, HALF], F32) for u in range(2)]
         out_bf = [sb(f"out_bf{u}", [P, HALF, PACK], BF16) for u in range(2)]
+        out_word = [sb(f"out_word{u}", [P, HALF], U32) for u in range(2)]
 
-        def finish_z(u, sum_bank, back_bank):
-            late = bank(sum_bank, [P, 1, P])
-            for d in range(2):
-                weigh(LAST, d, u * HALF, (u + 1) * HALF)
-                add_turned(late[:, 0, :], LAST, d, u)
-            round_turned(late, u, LAST, 1)
-            back = bank(back_bank, [P, 2, HALF])
-            pairs = zt_bf[u][:].rearrange("p k m e -> p (k m e)").bitcast(F32)
-            for k in range(2):
-                nc.tensor.transpose(back[:, k, :], pairs[:, block(k)], identity[:])
-            return back
-
-        def last_product(u, back, banks, copies):
-            nc.scalar.copy(
-                out=z_bf[u][:].rearrange("p v t -> p (v t)").bitcast(F32).rearrange("p (v k) -> p v k", k=2),
-                in_=back[:].rearrange("p k v -> p v k"),
+        for u in range(2):
+            nc.vector.tensor_tensor(
+                out=z_bf[u][:].rearrange("p (c i) j -> p c j i", i=4),
+                in0=term[:, 0, :, block(u)].rearrange("p j (c i) -> p c j i", i=4),
+                in1=term[:, 1, :, block(u)].rearrange("p j (c i) -> p c j i", i=4),
+                op=ADD,
             )
+        for u, banks, copies in [(0, [2], [nc.scalar.copy]), (1, [3, 0], [nc.vector.tensor_copy, nc.scalar.copy])]:
             nc.vector.quantize_mx(
                 out=z_word[u][:].bitcast(FP8X4), scales=z_scale[u][:], in_=z_bf[u][:].rearrange("p v t -> p (v t)")
             )
@@ -243,25 +264,16 @@ def tile_picked_zdin_sigmoid_po_kernel(
                     product(acc[:, s, :], w4_word[:, cols], w4_scale[:, cols], z_word[u][:], z_scale[u][:])
                 copy(out=out_sb[u][:, share * n : share * (n + 1), :], in_=acc[:])
             nc.sync.dma_start(out=out_rows[:, :, block(u)], in_=out_sb[u][:])
-
-        def hand_on(u):
-            interleave(nc.vector.tensor_copy, out_bf[u][:], out_sb[u][:])
-            out_word = sb(f"out_word{u}", [P, HALF], U32)
+        for u in range(2):
+            nc.vector.tensor_copy(
+                out=out_bf[u][:].rearrange("p (c i) j -> p c j i", i=4),
+                in_=out_sb[u][:].rearrange("p j (c i) -> p c j i", i=4),
+            )
             nc.vector.quantize_mx(
-                out=out_word[:].bitcast(FP8X4), scales=out_scale[:, block(u)],
+                out=out_word[u][:].bitcast(FP8X4), scales=out_scale[:, block(u)],
                 in_=out_bf[u][:].rearrange("p v t -> p (v t)"),
             )
-            nc.sync.dma_start(out=out_words[:, block(u)], in_=out_word[:].bitcast(I32))
-
-        backs = [finish_z(0, 5, 7), finish_z(1, 6, 1)]
-        w4_word = sb("w4_word", [P, N], U32, f"gate_slot{LAST}")
-        w4_scale = sb("w4_scale", [P, N], U8, f"logit_then_h{LAST - 1}")
-        deal(nc, w4_word, w4_raw, LINE // 4)
-        deal(nc, w4_scale, w4_scale_raw, LINE)
-        last_product(0, backs[0], [2], [nc.scalar.copy])
-        last_product(1, backs[1], [3, 0], [nc.vector.tensor_copy, nc.scalar.copy])
-        hand_on(0)
-        hand_on(1)
+            nc.sync.dma_start(out=out_words[:, block(u)], in_=out_word[u][:].bitcast(I32))
         for q in range(QUADS):
             queue = nc.sync if q % 2 == 0 else nc.scalar
             queue.dma_start(

@@ -109,9 +109,9 @@ def tile_picked_zdin_sigmoid_po_kernel(
         nc.scalar.activation(out=warm_out[:], in_=warm[:], func=SIGMOID)
         nc.sync.dma_start(offs_sb[:], offs)
         load_words(nc.sync, x_word, x_words)
+        nc.sync.dma_start(tgt_sb[:], tgt)
         load_words(nc.sync, w2_raw, w2_words)
         load_words(nc.sync, w1_raw, w1_words)
-        nc.sync.dma_start(tgt_sb[:], tgt)
         load_scales(nc.sync, w12_scale_raw, w2_scales, W2_ROW)
         load_scales(nc.sync, w12_scale_raw, w1_scales, 0, [LAST])
         nc.sync.dma_start(out=w3_raw[0][:], in_=w3_rows[:, :, : H // 2])
@@ -121,7 +121,6 @@ def tile_picked_zdin_sigmoid_po_kernel(
         load_words(nc.sync, w4_raw, w4_words)
         load_scales(nc.sync, w4_scale_raw, w4_scales, 0)
 
-        tgt_scale = sb("tgt_scale", [P, V], U8)
         hist_word = [sb(f"hist_word{u}", [P, V], U32) for u in range(2)]
         hist_scale = sb("hist_scale", [P, S], U8)
         w1_word = sb("w1_word", [P, N], U32)
@@ -132,11 +131,14 @@ def tile_picked_zdin_sigmoid_po_kernel(
             nc.vector.tensor_copy(out=hist_word[u][:], in_=x_word[:].indirect(offs_sb[:, 16 * u : 16 * (u + 1)]))
         deal(nc.gpsimd, w2_word, w2_raw, LINE // 4)
         deal(nc.gpsimd, w1_word, w1_raw, LINE // 4)
-        nc.vector.tensor_copy(out=tgt_scale[:], in_=x_scale[:].indirect(tgt_sb[:]))
+        tgt_scale = [sb("tgt_scale0", [P, HALF], U8)]
+        nc.vector.tensor_copy(out=tgt_scale[0][:], in_=x_scale[:].indirect(half_of(tgt_sb, 0)))
         deal(nc.vector, w12_scale, w12_scale_raw, LINE)
-        tgt_word = [placed(f"tgt_word{u}", [P, HALF], U32, 6144 + 512 * u) for u in range(2)]
-        for u in range(2):
-            nc.vector.tensor_copy(out=tgt_word[u][:], in_=x_word[:].indirect(half_of(tgt_sb, u)))
+        tgt_word = [placed("tgt_word0", [P, HALF], U32, 6144), placed("tgt_word1", [P, HALF], U32, 6144 + 640)]
+        tgt_scale.append(placed("tgt_scale1", [P, HALF], U8, 6144 + 512))
+        nc.vector.tensor_copy(out=tgt_word[0][:], in_=x_word[:].indirect(half_of(tgt_sb, 0)))
+        nc.vector.tensor_copy(out=tgt_scale[1][:], in_=x_scale[:].indirect(half_of(tgt_sb, 1)))
+        nc.vector.tensor_copy(out=tgt_word[1][:], in_=x_word[:].indirect(half_of(tgt_sb, 1)))
 
         def product(acc, word, scale, rhs_word, rhs_scale):
             nc.tensor.matmul_mx(
@@ -167,14 +169,14 @@ def tile_picked_zdin_sigmoid_po_kernel(
         def keys_and_targets(t):
             parts = [[0], [1]] if t == 0 else [[0, 1]]
             for part in parts:
-                acc = bank(max(t, part[0]), [P, len(part), V])
+                acc = bank(7 if t == 1 else max(t, part[0]), [P, len(part), V])
                 over_history(acc, part, w2_word[:, block(t)], w12_scale[W2_ROW:P, block(t)])
                 nc.scalar.copy(out=e_sb[t][:, part[0] * V : (part[-1] + 1) * V], in_=acc[:].rearrange("p n v -> p (n v)"))
             for part in parts:
                 acc = bank(2 + part[0] if t == 0 else LAST + t, [P, len(part), HALF])
                 for n, u in enumerate(part):
                     product(
-                        acc[:, n, :], w1_word[:, block(t)], w12_scale[:, block(t)], tgt_word[u][:], tgt_scale[:, block(u)]
+                        acc[:, n, :], w1_word[:, block(t)], w12_scale[:, block(t)], tgt_word[u][:], tgt_scale[u][:]
                     )
                 nc.scalar.copy(
                     out=y_sb[t][:, part[0] * HALF : (part[-1] + 1) * HALF], in_=acc[:].rearrange("p n v -> p (n v)")
@@ -213,10 +215,6 @@ def tile_picked_zdin_sigmoid_po_kernel(
         for t in range(2, TILES):
             keys_and_targets(t)
             logits(t)
-        w4_word = sb("w4_word", [P, N], U32)
-        w4_scale = sb("w4_scale", [P, N], U8)
-        deal(nc.vector, w4_word, w4_raw, LINE // 4)
-        deal(nc.vector, w4_scale, w4_scale_raw, LINE)
         for t in range(TILES):
             values(t)
             if t == 0:
@@ -224,15 +222,18 @@ def tile_picked_zdin_sigmoid_po_kernel(
             else:
                 gate[t] = sb(f"gate{t}", [P, 2, V], F32, "logit_slot0" if t == 1 else "")
             nc.scalar.activation(out=gate[t][:], in_=logit[t][:], func=SIGMOID)
-        picked = sb("picked", [P, 2, V], F32)
-        for d in range(2):
-            nc.scalar.activation(out=picked[:, d, :], in_=h_sb[LAST][:].indirect(pos_sb[d][:]), func=COPY)
+        picked = [sb(f"picked{u}", [P, 2, HALF], F32, f"picked_slot{u}") for u in range(2)]
+        for u in range(2):
+            for d in range(2):
+                nc.scalar.activation(
+                    out=picked[u][:, d, :], in_=h_sb[LAST][:].indirect(half_of(pos_sb[d], u)), func=COPY
+                )
         for t in range(LAST):
             for d in range(2):
                 weigh(t, d)
         for u in range(2):
             nc.vector.tensor_tensor(
-                out=term[:, :, LAST, block(u)], in0=picked[:, :, block(u)], in1=gate[LAST][:, :, block(u)], op=MULT
+                out=term[:, :, LAST, block(u)], in0=picked[u][:], in1=gate[LAST][:, :, block(u)], op=MULT
             )
 
         out_rows = out_0.rearrange("(p t) v -> p t v", t=PACK)
@@ -245,14 +246,22 @@ def tile_picked_zdin_sigmoid_po_kernel(
         out_bf = [sb(f"out_bf{u}", [P, HALF, PACK], BF16) for u in range(2)]
         out_word = [sb(f"out_word{u}", [P, HALF], U32) for u in range(2)]
 
-        for u in range(2):
+        def add_terms(u):
             nc.vector.tensor_tensor(
                 out=z_bf[u][:].rearrange("p (c i) j -> p c j i", i=4),
                 in0=term[:, 0, :, block(u)].rearrange("p j (c i) -> p c j i", i=4),
                 in1=term[:, 1, :, block(u)].rearrange("p j (c i) -> p c j i", i=4),
                 op=ADD,
             )
-        for u, banks, copies in [(0, [2], [nc.scalar.copy]), (1, [3, 0], [nc.vector.tensor_copy, nc.scalar.copy])]:
+
+        w4_word = sb("w4_word", [P, N], U32, "picked_slot0")
+        deal(nc.vector, w4_word, w4_raw, LINE // 4)
+        add_terms(0)
+        w4_scale = sb("w4_scale", [P, N], U8, "picked_slot1")
+        deal(nc.vector, w4_scale, w4_scale_raw, LINE)
+        for u, banks, copies in [(0, [2, 5], [nc.scalar.copy] * 2), (1, [3, 0], [nc.scalar.copy] * 2)]:
+            if u == 1:
+                add_terms(u)
             nc.vector.quantize_mx(
                 out=z_word[u][:].bitcast(FP8X4), scales=z_scale[u][:], in_=z_bf[u][:].rearrange("p v t -> p (v t)")
             )

@@ -85,10 +85,7 @@ def tile_picked_zdin_sigmoid_po_kernel(
         w4_raw = sb("w4_raw", [P, N], U32)
         w12_scale_raw = placed("w12_scale_raw", [P, N], U8, 6144 + 448)
         w4_scale_raw = sb("w4_scale_raw", [P, N], U8)
-        w3_raw = [
-            sb("w3_raw0", [P, PACK, H // 2], F32),
-            reuse.tile([P, PACK, H // 2], F32, name="w3_raw1", offset=1984, align_bytes=64),
-        ]
+        w3_raw = [sb(f"w3_raw{u}", [P, PACK, H // 2], F32) for u in range(2)]
         warm = sb("warm", [P, 8], F32)
         warm_out = sb("warm_out", [P, 8], F32)
 
@@ -110,14 +107,14 @@ def tile_picked_zdin_sigmoid_po_kernel(
         nc.sync.dma_start(offs_sb[:], offs)
         load_words(nc.sync, x_word, x_words)
         nc.sync.dma_start(tgt_sb[:], tgt)
+        nc.sync.dma_start(out=w3_raw[0][:], in_=w3_rows[:, :, : H // 2])
         load_words(nc.sync, w2_raw, w2_words)
-        load_words(nc.sync, w1_raw, w1_words)
         load_scales(nc.sync, w12_scale_raw, w2_scales, W2_ROW)
         load_scales(nc.sync, w12_scale_raw, w1_scales, 0, [LAST])
-        nc.sync.dma_start(out=w3_raw[0][:], in_=w3_rows[:, :, : H // 2])
+        load_words(nc.sync, w1_raw, w1_words)
+        nc.sync.dma_start(out=w3_raw[1][:], in_=w3_rows[:, :, H // 2 :])
         nc.sync.dma_start(pos_sb[0][:], pos1)
         nc.sync.dma_start(pos_sb[1][:], pos2)
-        nc.sync.dma_start(out=w3_raw[1][:], in_=w3_rows[:, :, H // 2 :])
         load_words(nc.sync, w4_raw, w4_words)
         load_scales(nc.sync, w4_scale_raw, w4_scales, 0)
 
@@ -147,7 +144,7 @@ def tile_picked_zdin_sigmoid_po_kernel(
             )
 
         y_sb = [sb(f"y_sb{t}", [P, V], F32) for t in range(TILES)]
-        e_sb = [sb(f"e_sb{t}", [P, S], F32) for t in range(2)]
+        e_sb = [sb(f"e_sb{t}", [P, S], F32) for t in range(TILES)]
         h_sb = {}
         logit = {}
         gate = {}
@@ -169,7 +166,7 @@ def tile_picked_zdin_sigmoid_po_kernel(
         def keys_and_targets(t):
             parts = [[0], [1]] if t == 0 else [[0, 1]]
             for part in parts:
-                acc = bank(7 if t == 1 else max(t, part[0]), [P, len(part), V])
+                acc = bank(max(t, part[0]), [P, len(part), V])
                 over_history(acc, part, w2_word[:, block(t)], w12_scale[W2_ROW:P, block(t)])
                 nc.scalar.copy(out=e_sb[t][:, part[0] * V : (part[-1] + 1) * V], in_=acc[:].rearrange("p n v -> p (n v)"))
             for part in parts:
@@ -202,26 +199,21 @@ def tile_picked_zdin_sigmoid_po_kernel(
                 out=term[:, d, t, :], in0=h_sb[t][:].indirect(pos_sb[d][:]), in1=gate[t][:, d, :], op=MULT,
             )
 
-        round_w3(0, nc.vector.tensor_copy)
-        for t in range(2):
-            keys_and_targets(t)
-            logits(t)
-        round_w3(1, nc.scalar.copy)
+        round_w3(0, nc.scalar.copy)
+        round_w3(1, nc.vector.tensor_copy)
         nc.vector.quantize_mx(
             out=w3_word[:].bitcast(FP8X4), scales=w3_scale[:], in_=w3_bf[:].rearrange("p t m j -> p (t m j)")
         )
-        e_sb.append(reuse.tile([P, S], F32, name="e_sb2", offset=4096, align_bytes=64))
-        e_sb.append(reuse.tile([P, S], F32, name="e_sb3", offset=0, align_bytes=64))
-        for t in range(2, TILES):
+        for t in range(TILES):
             keys_and_targets(t)
             logits(t)
         for t in range(TILES):
             values(t)
-            if t == 0:
-                gate[t] = placed("gate0", [P, 2, V], F32, 2048)
-            else:
-                gate[t] = sb(f"gate{t}", [P, 2, V], F32, "logit_slot0" if t == 1 else "")
+            gate[t] = sb(f"gate{t}", [P, 2, V], F32)
             nc.scalar.activation(out=gate[t][:], in_=logit[t][:], func=SIGMOID)
+            if t == 2:
+                picked2 = sb("picked2", [P, V], F32)
+                nc.scalar.activation(out=picked2[:], in_=h_sb[t][:].indirect(pos_sb[1][:]), func=COPY)
         picked = [sb(f"picked{u}", [P, 2, HALF], F32, f"picked_slot{u}") for u in range(2)]
         for u in range(2):
             for d in range(2):
@@ -229,8 +221,10 @@ def tile_picked_zdin_sigmoid_po_kernel(
                     out=picked[u][:, d, :], in_=h_sb[LAST][:].indirect(half_of(pos_sb[d], u)), func=COPY
                 )
         for t in range(LAST):
-            for d in range(2):
-                weigh(t, d)
+            weigh(t, 0)
+            if t < 2:
+                weigh(t, 1)
+        nc.vector.tensor_tensor(out=term[:, 1, 2, :], in0=picked2[:], in1=gate[2][:, 1, :], op=MULT)
         for u in range(2):
             nc.vector.tensor_tensor(
                 out=term[:, :, LAST, block(u)], in0=picked[u][:], in1=gate[LAST][:, :, block(u)], op=MULT

@@ -24,7 +24,6 @@ TILES = 4
 LAST = TILES - 1
 HALF = V // 2
 LINE = 16
-W2_ROW = 4
 
 
 def block(n):
@@ -39,10 +38,10 @@ def load_words(queue, tile, words):
     queue.dma_start(out=tile[:].bitcast(I32), in_=words[0].rearrange("p n t -> p (n t)").bitcast(I32))
 
 
-def load_scales(queue, tile, scales, row, quads=range(QUADS)):
+def load_scales(queue, tile, scales, quads=range(QUADS)):
     for q in quads:
         queue.dma_start(
-            out=tile[32 * q + row : 32 * q + row + 4, :].bitcast(I32),
+            out=tile[32 * q : 32 * q + 4, :].bitcast(I32),
             in_=scales[0, 4 * q : 4 * q + 4, :].bitcast(I32),
         )
 
@@ -83,15 +82,17 @@ def tile_picked_zdin_sigmoid_po_kernel(
         w1_raw = sb("w1_raw", [P, N], U32)
         w2_raw = sb("w2_raw", [P, N], U32)
         w4_raw = sb("w4_raw", [P, N], U32)
-        w12_scale_raw = placed("w12_scale_raw", [P, N], U8, 6144 + 448)
+        w1_scale_raw = sb("w1_scale_raw", [P, N], U8)
+        w2_scale_raw = placed("w2_scale_raw", [P, N], U8, 448)
         w4_scale_raw = sb("w4_scale_raw", [P, N], U8)
         w3_raw = [sb(f"w3_raw{u}", [P, PACK, H // 2], F32) for u in range(2)]
         warm = sb("warm", [P, 8], F32)
         warm_out = sb("warm_out", [P, 8], F32)
 
-        nc.gpsimd.memset(w12_scale_raw[:].bitcast(I32), 0)
-        load_scales(nc.gpsimd, w12_scale_raw, w1_scales, 0, range(LAST))
+        nc.gpsimd.memset(w1_scale_raw[:].bitcast(I32), 0)
+        load_scales(nc.gpsimd, w1_scale_raw, w1_scales, range(2))
         nc.vector.memset(warm[:], 0.0)
+        nc.vector.memset(w2_scale_raw[:].bitcast(I32), 0)
         nc.vector.memset(w4_scale_raw[:].bitcast(I32), 0)
 
         def load_x_scale(queue, q):
@@ -108,34 +109,35 @@ def tile_picked_zdin_sigmoid_po_kernel(
         load_words(nc.sync, x_word, x_words)
         nc.sync.dma_start(tgt_sb[:], tgt)
         nc.sync.dma_start(out=w3_raw[0][:], in_=w3_rows[:, :, : H // 2])
+        load_scales(nc.sync, w2_scale_raw, w2_scales)
         load_words(nc.sync, w2_raw, w2_words)
-        load_scales(nc.sync, w12_scale_raw, w2_scales, W2_ROW)
-        load_scales(nc.sync, w12_scale_raw, w1_scales, 0, [LAST])
         load_words(nc.sync, w1_raw, w1_words)
+        load_scales(nc.sync, w1_scale_raw, w1_scales, range(2, QUADS))
         nc.sync.dma_start(out=w3_raw[1][:], in_=w3_rows[:, :, H // 2 :])
         nc.sync.dma_start(pos_sb[0][:], pos1)
         nc.sync.dma_start(pos_sb[1][:], pos2)
         load_words(nc.sync, w4_raw, w4_words)
-        load_scales(nc.sync, w4_scale_raw, w4_scales, 0)
+        load_scales(nc.sync, w4_scale_raw, w4_scales)
 
-        hist_word = [sb(f"hist_word{u}", [P, V], U32) for u in range(2)]
+        hist_word = sb("hist_word", [P, S], U32)
         hist_scale = sb("hist_scale", [P, S], U8)
         w1_word = sb("w1_word", [P, N], U32)
         w2_word = sb("w2_word", [P, N], U32)
-        w12_scale = sb("w12_scale", [P, N], U8)
+        w1_scale = sb("w1_scale", [P, N], U8)
+        w2_scale = sb("w2_scale", [P, N], U8)
         nc.vector.tensor_copy(out=hist_scale[:], in_=x_scale[:].indirect(offs_sb[:]))
-        for u in range(2):
-            nc.vector.tensor_copy(out=hist_word[u][:], in_=x_word[:].indirect(offs_sb[:, 16 * u : 16 * (u + 1)]))
+        nc.vector.tensor_copy(out=hist_word[:], in_=x_word[:].indirect(offs_sb[:]))
         deal(nc.gpsimd, w2_word, w2_raw, LINE // 4)
         deal(nc.gpsimd, w1_word, w1_raw, LINE // 4)
         tgt_scale = [sb("tgt_scale0", [P, HALF], U8)]
         nc.vector.tensor_copy(out=tgt_scale[0][:], in_=x_scale[:].indirect(half_of(tgt_sb, 0)))
-        deal(nc.vector, w12_scale, w12_scale_raw, LINE)
-        tgt_word = [placed("tgt_word0", [P, HALF], U32, 6144), placed("tgt_word1", [P, HALF], U32, 6144 + 640)]
-        tgt_scale.append(placed("tgt_scale1", [P, HALF], U8, 6144 + 512))
+        deal(nc.vector, w2_scale, w2_scale_raw, LINE)
+        tgt_word = [placed("tgt_word0", [P, HALF], U32, 0), placed("tgt_word1", [P, HALF], U32, 640)]
+        tgt_scale.append(placed("tgt_scale1", [P, HALF], U8, 512))
         nc.vector.tensor_copy(out=tgt_word[0][:], in_=x_word[:].indirect(half_of(tgt_sb, 0)))
         nc.vector.tensor_copy(out=tgt_scale[1][:], in_=x_scale[:].indirect(half_of(tgt_sb, 1)))
         nc.vector.tensor_copy(out=tgt_word[1][:], in_=x_word[:].indirect(half_of(tgt_sb, 1)))
+        deal(nc.vector, w1_scale, w1_scale_raw, LINE)
 
         def product(acc, word, scale, rhs_word, rhs_scale):
             nc.tensor.matmul_mx(
@@ -144,7 +146,7 @@ def tile_picked_zdin_sigmoid_po_kernel(
             )
 
         y_sb = [sb(f"y_sb{t}", [P, V], F32) for t in range(TILES)]
-        e_sb = [sb(f"e_sb{t}", [P, S], F32) for t in range(TILES)]
+        e_sb = {}
         h_sb = {}
         logit = {}
         gate = {}
@@ -159,28 +161,32 @@ def tile_picked_zdin_sigmoid_po_kernel(
                 in_=w3_raw[u][:].rearrange("p j (c i t) -> p c j i t", i=2, t=PACK),
             )
 
-        def over_history(acc, part, word, scale):
-            for n, u in enumerate(part):
-                product(acc[:, n, :], word, scale, hist_word[u][:], hist_scale[:, u * V : (u + 1) * V])
+        def parts_of(t):
+            return [[0], [1]] if t == 0 else [[0, 1]]
 
-        def keys_and_targets(t):
-            parts = [[0], [1]] if t == 0 else [[0, 1]]
-            for part in parts:
-                acc = bank(max(t, part[0]), [P, len(part), V])
-                over_history(acc, part, w2_word[:, block(t)], w12_scale[W2_ROW:P, block(t)])
-                nc.scalar.copy(out=e_sb[t][:, part[0] * V : (part[-1] + 1) * V], in_=acc[:].rearrange("p n v -> p (n v)"))
-            for part in parts:
+        def key_products(t):
+            acc = bank(t, [P, 1, S])
+            product(acc[:, 0, :], w2_word[:, block(t)], w2_scale[:, block(t)], hist_word[:], hist_scale[:])
+            return [acc]
+
+        def target_products(t):
+            accs = []
+            for part in parts_of(t):
                 acc = bank(2 + part[0] if t == 0 else LAST + t, [P, len(part), HALF])
                 for n, u in enumerate(part):
                     product(
-                        acc[:, n, :], w1_word[:, block(t)], w12_scale[:, block(t)], tgt_word[u][:], tgt_scale[u][:]
+                        acc[:, n, :], w1_word[:, block(t)], w1_scale[:, block(t)], tgt_word[u][:], tgt_scale[u][:]
                     )
-                nc.scalar.copy(
-                    out=y_sb[t][:, part[0] * HALF : (part[-1] + 1) * HALF], in_=acc[:].rearrange("p n v -> p (n v)")
-                )
+                accs.append(acc)
+            return accs
+
+        def empty(accs, rows):
+            width = rows.shape[1] // len(accs)
+            for n, acc in enumerate(accs):
+                nc.scalar.copy(out=rows[:, n * width : (n + 1) * width], in_=acc[:].rearrange("p n v -> p (n v)"))
 
         def logits(t):
-            logit[t] = sb(f"logit{t}", [P, 2, V], F32, f"logit_slot{t}")
+            logit[t] = sb(f"logit{t}", [P, 2, V], F32)
             for lo, hi in [(0, HALF), (HALF, V)] if t == 0 else [(0, V)]:
                 for d in range(2):
                     nc.vector.tensor_tensor(
@@ -190,9 +196,9 @@ def tile_picked_zdin_sigmoid_po_kernel(
 
         def values(t):
             h_sb[t] = sb(f"h_sb{t}", [P, S], F32)
-            acc = bank([6, 0, 7, 4][t], [P, 2, V])
-            over_history(acc, [0, 1], w3_word[:, block(t)], w3_scale[:, block(t)])
-            nc.scalar.copy(out=h_sb[t][:], in_=acc[:].rearrange("p n v -> p (n v)"))
+            acc = bank([6, 0, 7, 4][t], [P, S])
+            product(acc[:], w3_word[:, block(t)], w3_scale[:, block(t)], hist_word[:], hist_scale[:])
+            nc.scalar.copy(out=h_sb[t][:], in_=acc[:])
 
         def weigh(t, d):
             nc.vector.tensor_tensor(
@@ -204,8 +210,12 @@ def tile_picked_zdin_sigmoid_po_kernel(
         nc.vector.quantize_mx(
             out=w3_word[:].bitcast(FP8X4), scales=w3_scale[:], in_=w3_bf[:].rearrange("p t m j -> p (t m j)")
         )
+        keys = {t: key_products(t) for t in range(2)}
+        targets = [target_products(t) for t in range(TILES)]
         for t in range(TILES):
-            keys_and_targets(t)
+            e_sb[t] = placed("e_sb1", [P, S], F32, 0) if t == 1 else sb(f"e_sb{t}", [P, S], F32)
+            empty(keys[t] if t in keys else key_products(t), e_sb[t][:])
+            empty(targets[t], y_sb[t][:])
             logits(t)
         for t in range(TILES):
             values(t)

@@ -90,7 +90,7 @@ def tile_picked_zdin_sigmoid_po_kernel(
         warm_out = sb("warm_out", [P, 8], F32)
 
         nc.gpsimd.memset(w1_scale_raw[:].bitcast(I32), 0)
-        load_scales(nc.gpsimd, w1_scale_raw, w1_scales, range(2))
+        load_scales(nc.gpsimd, w1_scale_raw, w1_scales, range(LAST))
         nc.vector.memset(warm[:], 0.0)
         nc.vector.memset(w2_scale_raw[:].bitcast(I32), 0)
         nc.vector.memset(w4_scale_raw[:].bitcast(I32), 0)
@@ -112,7 +112,7 @@ def tile_picked_zdin_sigmoid_po_kernel(
         load_scales(nc.sync, w2_scale_raw, w2_scales)
         load_words(nc.sync, w2_raw, w2_words)
         load_words(nc.sync, w1_raw, w1_words)
-        load_scales(nc.sync, w1_scale_raw, w1_scales, range(2, QUADS))
+        load_scales(nc.sync, w1_scale_raw, w1_scales, [LAST])
         nc.sync.dma_start(out=w3_raw[1][:], in_=w3_rows[:, :, H // 2 :])
         nc.sync.dma_start(pos_sb[0][:], pos1)
         nc.sync.dma_start(pos_sb[1][:], pos2)
@@ -129,14 +129,12 @@ def tile_picked_zdin_sigmoid_po_kernel(
         nc.vector.tensor_copy(out=hist_word[:], in_=x_word[:].indirect(offs_sb[:]))
         deal(nc.gpsimd, w2_word, w2_raw, LINE // 4)
         deal(nc.gpsimd, w1_word, w1_raw, LINE // 4)
-        tgt_scale = [sb("tgt_scale0", [P, HALF], U8)]
-        nc.vector.tensor_copy(out=tgt_scale[0][:], in_=x_scale[:].indirect(half_of(tgt_sb, 0)))
         deal(nc.vector, w2_scale, w2_scale_raw, LINE)
-        tgt_word = [placed("tgt_word0", [P, HALF], U32, 0), placed("tgt_word1", [P, HALF], U32, 640)]
-        tgt_scale.append(placed("tgt_scale1", [P, HALF], U8, 512))
-        nc.vector.tensor_copy(out=tgt_word[0][:], in_=x_word[:].indirect(half_of(tgt_sb, 0)))
-        nc.vector.tensor_copy(out=tgt_scale[1][:], in_=x_scale[:].indirect(half_of(tgt_sb, 1)))
-        nc.vector.tensor_copy(out=tgt_word[1][:], in_=x_word[:].indirect(half_of(tgt_sb, 1)))
+        tgt_scale = [placed(f"tgt_scale{u}", [P, HALF], U8, 512 + 128 * u) for u in range(2)]
+        tgt_word = [placed(f"tgt_word{u}", [P, HALF], U32, 768 * u) for u in range(2)]
+        for u in range(2):
+            nc.vector.tensor_copy(out=tgt_scale[u][:], in_=x_scale[:].indirect(half_of(tgt_sb, u)))
+            nc.vector.tensor_copy(out=tgt_word[u][:], in_=x_word[:].indirect(half_of(tgt_sb, u)))
         deal(nc.vector, w1_scale, w1_scale_raw, LINE)
 
         def product(acc, word, scale, rhs_word, rhs_scale):

@@ -24,6 +24,7 @@ TILES = 4
 LAST = TILES - 1
 HALF = V // 2
 LINE = 16
+W3_PARTS = [(0, 128), (128, 256), (256, 512)]
 
 
 def block(n):
@@ -46,8 +47,15 @@ def load_scales(queue, tile, scales, quads=range(QUADS)):
         )
 
 
-def deal(engine, dealt, raw, run):
-    engine.tensor_copy(
+def load_repeated(queue, tile, scales, q):
+    rows = scales[0, 4 * q : 4 * q + 4, :].bitcast(I32)
+    queue.dma_start(
+        out=tile[32 * q : 32 * (q + 1), :].bitcast(I32), in_=rows.unsqueeze(0).broadcast_to([8, 4, rows.shape[1]])
+    )
+
+
+def deal(copy, dealt, raw, run):
+    copy(
         out=dealt[:].rearrange("p (t c i) -> p c t i", t=PACK, i=run),
         in_=raw[:].rearrange("p (c i t) -> p c t i", t=PACK, i=run),
     )
@@ -61,7 +69,6 @@ def tile_picked_zdin_sigmoid_po_kernel(
     with ExitStack() as ctx:
         lists = ctx.enter_context(tc.tile_pool(name="lists", bufs=1))
         keep = ctx.enter_context(tc.tile_pool(name="keep", bufs=1))
-        reuse = ctx.enter_context(tc.tile_pool(name="reuse", bufs=1))
         psum = ctx.enter_context(tc.psum_pool(name="psum", bufs=1))
 
         offs_sb = lists.tile([P, S // 16], U16, name="offs_sb")
@@ -70,9 +77,6 @@ def tile_picked_zdin_sigmoid_po_kernel(
 
         def sb(name, shape, dtype, tag=""):
             return keep.tile(shape, dtype, name=name, tag=tag, align_bytes=64)
-
-        def placed(name, shape, dtype, offset):
-            return reuse.tile(shape, dtype, name=name, offset=offset, align_bytes=64)
 
         def bank(number, shape):
             return psum.tile(shape, F32, name="acc", tag=f"bank{number}")
@@ -83,59 +87,57 @@ def tile_picked_zdin_sigmoid_po_kernel(
         w2_raw = sb("w2_raw", [P, N], U32)
         w4_raw = sb("w4_raw", [P, N], U32)
         w1_scale_raw = sb("w1_scale_raw", [P, N], U8)
-        w2_scale_raw = placed("w2_scale_raw", [P, N], U8, 448)
         w4_scale_raw = sb("w4_scale_raw", [P, N], U8)
-        w3_raw = [sb(f"w3_raw{u}", [P, PACK, H // 2], F32) for u in range(2)]
+        w2_scale_raw = sb("w2_scale_raw", [P, N], U8, "w2_scale_slot")
+        w3_raw = [sb(f"w3_raw{n}", [P, PACK, hi - lo], F32, f"w3_slot{n}") for n, (lo, hi) in enumerate(W3_PARTS)]
         warm = sb("warm", [P, 8], F32)
         warm_out = sb("warm_out", [P, 8], F32)
 
-        nc.gpsimd.memset(w1_scale_raw[:].bitcast(I32), 0)
-        load_scales(nc.gpsimd, w1_scale_raw, w1_scales, range(LAST))
+        for q in range(LAST):
+            load_repeated(nc.gpsimd, w1_scale_raw, w1_scales, q)
         nc.vector.memset(warm[:], 0.0)
         nc.vector.memset(w2_scale_raw[:].bitcast(I32), 0)
         nc.vector.memset(w4_scale_raw[:].bitcast(I32), 0)
 
-        def load_x_scale(queue, q):
-            queue.dma_start(
-                out=x_scale[32 * q : 32 * (q + 1), :].bitcast(I32),
-                in_=x_scales[0, 4 * q : 4 * q + 4, :].bitcast(I32).unsqueeze(0).broadcast_to([8, 4, T // 4]),
-            )
-
         w3_rows = w3.rearrange("(p j) c -> p j c", j=PACK)
-        for q in range(QUADS):
-            load_x_scale(nc.sync if q < QUADS // 2 else nc.scalar, q)
-        nc.scalar.activation(out=warm_out[:], in_=warm[:], func=SIGMOID)
         nc.sync.dma_start(offs_sb[:], offs)
-        load_words(nc.sync, x_word, x_words)
+        for q in range(QUADS):
+            load_repeated(nc.sync if q < QUADS // 2 else nc.scalar, x_scale, x_scales, q)
+        nc.scalar.activation(out=warm_out[:], in_=warm[:], func=SIGMOID)
+
+        def load_w3(n):
+            nc.sync.dma_start(out=w3_raw[n][:], in_=w3_rows[:, :, W3_PARTS[n][0] : W3_PARTS[n][1]])
+
         nc.sync.dma_start(tgt_sb[:], tgt)
-        nc.sync.dma_start(out=w3_raw[0][:], in_=w3_rows[:, :, : H // 2])
+        load_w3(0)
+        load_words(nc.sync, x_word, x_words)
         load_scales(nc.sync, w2_scale_raw, w2_scales)
         load_words(nc.sync, w2_raw, w2_words)
         load_words(nc.sync, w1_raw, w1_words)
-        load_scales(nc.sync, w1_scale_raw, w1_scales, [LAST])
-        nc.sync.dma_start(out=w3_raw[1][:], in_=w3_rows[:, :, H // 2 :])
+        load_w3(1)
+        load_repeated(nc.sync, w1_scale_raw, w1_scales, LAST)
+        load_w3(2)
         nc.sync.dma_start(pos_sb[0][:], pos1)
         nc.sync.dma_start(pos_sb[1][:], pos2)
         load_words(nc.sync, w4_raw, w4_words)
         load_scales(nc.sync, w4_scale_raw, w4_scales)
 
-        hist_word = sb("hist_word", [P, S], U32)
         hist_scale = sb("hist_scale", [P, S], U8)
+        tgt_scale = sb("tgt_scale", [P, V], U8)
         w1_word = sb("w1_word", [P, N], U32)
         w2_word = sb("w2_word", [P, N], U32)
         w1_scale = sb("w1_scale", [P, N], U8)
         w2_scale = sb("w2_scale", [P, N], U8)
         nc.vector.tensor_copy(out=hist_scale[:], in_=x_scale[:].indirect(offs_sb[:]))
+        nc.vector.tensor_copy(out=tgt_scale[:], in_=x_scale[:].indirect(tgt_sb[:]))
+        hist_word = sb("hist_word", [P, S], U32)
         nc.vector.tensor_copy(out=hist_word[:], in_=x_word[:].indirect(offs_sb[:]))
-        deal(nc.gpsimd, w2_word, w2_raw, LINE // 4)
-        deal(nc.gpsimd, w1_word, w1_raw, LINE // 4)
-        deal(nc.vector, w2_scale, w2_scale_raw, LINE)
-        tgt_scale = [placed(f"tgt_scale{u}", [P, HALF], U8, 512 + 128 * u) for u in range(2)]
-        tgt_word = [placed(f"tgt_word{u}", [P, HALF], U32, 768 * u) for u in range(2)]
-        for u in range(2):
-            nc.vector.tensor_copy(out=tgt_scale[u][:], in_=x_scale[:].indirect(half_of(tgt_sb, u)))
-            nc.vector.tensor_copy(out=tgt_word[u][:], in_=x_word[:].indirect(half_of(tgt_sb, u)))
-        deal(nc.vector, w1_scale, w1_scale_raw, LINE)
+        deal(nc.vector.tensor_copy, w2_scale, w2_scale_raw, LINE)
+        tgt_word = sb("tgt_word", [P, V], U32, "w2_scale_slot")
+        nc.vector.tensor_copy(out=tgt_word[:], in_=x_word[:].indirect(tgt_sb[:]))
+        deal(nc.scalar.copy, w2_word, w2_raw, LINE // 4)
+        deal(nc.scalar.copy, w1_word, w1_raw, LINE // 4)
+        deal(nc.vector.tensor_copy, w1_scale, w1_scale_raw, LINE)
 
         def product(acc, word, scale, rhs_word, rhs_scale):
             nc.tensor.matmul_mx(
@@ -143,100 +145,76 @@ def tile_picked_zdin_sigmoid_po_kernel(
                 rhs=rhs_word.bitcast(FP8X4), rhs_scale=rhs_scale, start=True, stop=True,
             )
 
-        y_sb = [sb(f"y_sb{t}", [P, V], F32) for t in range(TILES)]
-        e_sb = {}
-        h_sb = {}
-        logit = {}
-        gate = {}
-        term = sb("term", [P, 2, TILES, V], F32)
         w3_bf = sb("w3_bf", [P, TILES, P, PACK], BF16)
         w3_word = sb("w3_word", [P, H], U32)
         w3_scale = sb("w3_scale", [P, H], U8)
-
-        def round_w3(u, copy):
+        for n, copy in enumerate([nc.scalar.copy, nc.scalar.copy, nc.vector.tensor_copy]):
+            lo, hi = W3_PARTS[n]
             copy(
-                out=w3_bf[:, :, 64 * u : 64 * (u + 1), :].rearrange("p t (c i) j -> p c j i t", i=2),
-                in_=w3_raw[u][:].rearrange("p j (c i t) -> p c j i t", i=2, t=PACK),
+                out=w3_bf[:, :, lo // PACK : hi // PACK, :].rearrange("p t (c i) j -> p c j i t", i=2),
+                in_=w3_raw[n][:].rearrange("p j (c i t) -> p c j i t", i=2, t=PACK),
             )
 
-        def parts_of(t):
-            return [[0], [1]] if t == 0 else [[0, 1]]
+        def key_product(t):
+            acc = bank(t, [P, S])
+            product(acc[:], w2_word[:, block(t)], w2_scale[:, block(t)], hist_word[:], hist_scale[:])
+            return acc
 
-        def key_products(t):
-            acc = bank(t, [P, 1, S])
-            product(acc[:, 0, :], w2_word[:, block(t)], w2_scale[:, block(t)], hist_word[:], hist_scale[:])
-            return [acc]
+        def rows_of(word, scale, t, number, name):
+            acc = bank(number, [P, S])
+            product(acc[:], word[:, block(t)], scale[:, block(t)], hist_word[:], hist_scale[:])
+            rows = sb(name, [P, S], F32)
+            nc.scalar.copy(out=rows[:], in_=acc[:])
+            return rows
 
-        def target_products(t):
-            accs = []
-            for part in parts_of(t):
-                acc = bank(2 + part[0] if t == 0 else LAST + t, [P, len(part), HALF])
-                for n, u in enumerate(part):
-                    product(
-                        acc[:, n, :], w1_word[:, block(t)], w1_scale[:, block(t)], tgt_word[u][:], tgt_scale[u][:]
-                    )
-                accs.append(acc)
-            return accs
-
-        def empty(accs, rows):
-            width = rows.shape[1] // len(accs)
-            for n, acc in enumerate(accs):
-                nc.scalar.copy(out=rows[:, n * width : (n + 1) * width], in_=acc[:].rearrange("p n v -> p (n v)"))
-
-        def logits(t):
-            logit[t] = sb(f"logit{t}", [P, 2, V], F32)
-            for lo, hi in [(0, HALF), (HALF, V)] if t == 0 else [(0, V)]:
+        logit = []
+        keys_acc = [key_product(t) for t in range(2)]
+        targets = []
+        for t in range(TILES):
+            targets.append(bank([2, 3, 5, 4][t], [P, V]))
+            product(targets[t][:], w1_word[:, block(t)], w1_scale[:, block(t)], tgt_word[:], tgt_scale[:])
+        for t in range(TILES):
+            e_sb = sb(f"e_sb{t}", [P, S], F32, ["w3_slot1", "w2_scale_slot", "", ""][t])
+            nc.scalar.copy(out=e_sb[:], in_=(keys_acc[t] if t < 2 else key_product(t))[:])
+            y_acc = targets[t]
+            logit.append(sb(f"logit{t}", [P, 2, V], F32, "last_logits" if t == LAST else ""))
+            if t < LAST:
+                y_sb = sb(f"y_sb{t}", [P, V], F32)
+                nc.scalar.copy(out=y_sb[:], in_=y_acc[:])
                 for d in range(2):
                     nc.vector.tensor_tensor(
-                        out=logit[t][:, d, lo:hi], in0=e_sb[t][:].indirect(pos_sb[d][:, lo // 16 : hi // 16]),
-                        in1=y_sb[t][:, lo:hi], op=MULT,
+                        out=logit[t][:, d, :], in0=e_sb[:].indirect(pos_sb[d][:]), in1=y_sb[:], op=MULT
                     )
-
-        def values(t):
-            h_sb[t] = sb(f"h_sb{t}", [P, S], F32)
-            acc = bank([6, 0, 7, 4][t], [P, S])
-            product(acc[:], w3_word[:, block(t)], w3_scale[:, block(t)], hist_word[:], hist_scale[:])
-            nc.scalar.copy(out=h_sb[t][:], in_=acc[:])
-
-        def weigh(t, d):
-            nc.vector.tensor_tensor(
-                out=term[:, d, t, :], in0=h_sb[t][:].indirect(pos_sb[d][:]), in1=gate[t][:, d, :], op=MULT,
-            )
-
-        round_w3(0, nc.scalar.copy)
-        round_w3(1, nc.vector.tensor_copy)
-        nc.vector.quantize_mx(
-            out=w3_word[:].bitcast(FP8X4), scales=w3_scale[:], in_=w3_bf[:].rearrange("p t m j -> p (t m j)")
-        )
-        keys = {t: key_products(t) for t in range(2)}
-        targets = [target_products(t) for t in range(TILES)]
-        for t in range(TILES):
-            e_sb[t] = placed("e_sb1", [P, S], F32, 0) if t == 1 else sb(f"e_sb{t}", [P, S], F32)
-            empty(keys[t] if t in keys else key_products(t), e_sb[t][:])
-            empty(targets[t], y_sb[t][:])
-            logits(t)
-        for t in range(TILES):
-            values(t)
-            gate[t] = sb(f"gate{t}", [P, 2, V], F32)
-            nc.scalar.activation(out=gate[t][:], in_=logit[t][:], func=SIGMOID)
-            if t == 2:
-                picked2 = sb("picked2", [P, V], F32)
-                nc.scalar.activation(out=picked2[:], in_=h_sb[t][:].indirect(pos_sb[1][:]), func=COPY)
-        picked = [sb(f"picked{u}", [P, 2, HALF], F32, f"picked_slot{u}") for u in range(2)]
-        for u in range(2):
-            for d in range(2):
-                nc.scalar.activation(
-                    out=picked[u][:, d, :], in_=h_sb[LAST][:].indirect(half_of(pos_sb[d], u)), func=COPY
+                    if t == 0 and d == 0:
+                        nc.vector.quantize_mx(
+                            out=w3_word[:].bitcast(FP8X4), scales=w3_scale[:],
+                            in_=w3_bf[:].rearrange("p t m j -> p (t m j)"),
+                        )
+            else:
+                keys = sb("keys", [P, 2, V], F32)
+                for d in range(2):
+                    nc.scalar.activation(out=keys[:, d, :], in_=e_sb[:].indirect(pos_sb[d][:]), func=COPY)
+                nc.vector.tensor_tensor(
+                    out=logit[t][:], in0=keys[:], in1=y_acc[:].unsqueeze(1).broadcast_to([P, 2, V]), op=MULT
                 )
-        for t in range(LAST):
-            weigh(t, 0)
-            if t < 2:
-                weigh(t, 1)
-        nc.vector.tensor_tensor(out=term[:, 1, 2, :], in0=picked2[:], in1=gate[2][:, 1, :], op=MULT)
+
+        term = sb("term", [P, 2, TILES, V], F32)
+        for t in range(TILES):
+            h_sb = rows_of(w3_word, w3_scale, t, [6, 7, 0, 1][t], f"h_sb{t}")
+            gate = sb(f"gate{t}", [P, 2, V], F32)
+            nc.scalar.activation(out=gate[:], in_=logit[t][:], func=SIGMOID)
+            for d in range(2 if t < LAST else 1):
+                nc.vector.tensor_tensor(
+                    out=term[:, d, t, :], in0=h_sb[:].indirect(pos_sb[d][:]), in1=gate[:, d, :], op=MULT
+                )
+        picked = sb("picked", [P, V], F32, "picked_slot")
+        nc.scalar.activation(out=picked[:], in_=h_sb[:].indirect(pos_sb[1][:]), func=COPY)
         for u in range(2):
             nc.vector.tensor_tensor(
-                out=term[:, :, LAST, block(u)], in0=picked[u][:], in1=gate[LAST][:, :, block(u)], op=MULT
+                out=term[:, 1, LAST, block(u)], in0=picked[:, block(u)], in1=gate[:, 1, block(u)], op=MULT
             )
+        w4_word = sb("w4_word", [P, N], U32, "last_logits")
+        deal(nc.scalar.copy, w4_word, w4_raw, LINE // 4)
 
         out_rows = out_0.rearrange("(p t) v -> p t v", t=PACK)
         out_words = out_1[0].rearrange("p v t -> p (v t)").bitcast(I32)
@@ -247,33 +225,25 @@ def tile_picked_zdin_sigmoid_po_kernel(
         out_sb = [sb(f"out_sb{u}", [P, PACK, HALF], F32) for u in range(2)]
         out_bf = [sb(f"out_bf{u}", [P, HALF, PACK], BF16) for u in range(2)]
         out_word = [sb(f"out_word{u}", [P, HALF], U32) for u in range(2)]
-
-        def add_terms(u):
+        for u in range(2):
             nc.vector.tensor_tensor(
                 out=z_bf[u][:].rearrange("p (c i) j -> p c j i", i=4),
                 in0=term[:, 0, :, block(u)].rearrange("p j (c i) -> p c j i", i=4),
                 in1=term[:, 1, :, block(u)].rearrange("p j (c i) -> p c j i", i=4),
                 op=ADD,
             )
-
-        w4_word = sb("w4_word", [P, N], U32, "picked_slot0")
-        deal(nc.vector, w4_word, w4_raw, LINE // 4)
-        add_terms(0)
-        w4_scale = sb("w4_scale", [P, N], U8, "picked_slot1")
-        deal(nc.vector, w4_scale, w4_scale_raw, LINE)
-        for u, banks, copies in [(0, [2, 5], [nc.scalar.copy] * 2), (1, [3, 0], [nc.scalar.copy] * 2)]:
-            if u == 1:
-                add_terms(u)
+            if u == 0:
+                w4_scale = sb("w4_scale", [P, N], U8, "picked_slot")
+                deal(nc.vector.tensor_copy, w4_scale, w4_scale_raw, LINE)
             nc.vector.quantize_mx(
                 out=z_word[u][:].bitcast(FP8X4), scales=z_scale[u][:], in_=z_bf[u][:].rearrange("p v t -> p (v t)")
             )
-            share = PACK // len(copies)
-            for n, copy in enumerate(copies):
-                acc = bank(banks[n], [P, share, HALF])
-                for s in range(share):
-                    cols = block(share * n + s)
+            for n in range(2):
+                acc = bank([[2, 3], [5, 6]][u][n], [P, 2, HALF])
+                for s in range(2):
+                    cols = block(2 * n + s)
                     product(acc[:, s, :], w4_word[:, cols], w4_scale[:, cols], z_word[u][:], z_scale[u][:])
-                copy(out=out_sb[u][:, share * n : share * (n + 1), :], in_=acc[:])
+                nc.scalar.copy(out=out_sb[u][:, 2 * n : 2 * (n + 1), :], in_=acc[:])
             nc.sync.dma_start(out=out_rows[:, :, block(u)], in_=out_sb[u][:])
         for u in range(2):
             nc.vector.tensor_copy(

@@ -69,6 +69,7 @@ def tile_picked_zdin_sigmoid_po_kernel(
     with ExitStack() as ctx:
         lists = ctx.enter_context(tc.tile_pool(name="lists", bufs=1))
         keep = ctx.enter_context(tc.tile_pool(name="keep", bufs=1))
+        reuse = ctx.enter_context(tc.tile_pool(name="reuse", bufs=1))
         psum = ctx.enter_context(tc.psum_pool(name="psum", bufs=1))
 
         offs_sb = lists.tile([P, S // 16], U16, name="offs_sb")
@@ -78,17 +79,20 @@ def tile_picked_zdin_sigmoid_po_kernel(
         def sb(name, shape, dtype, tag=""):
             return keep.tile(shape, dtype, name=name, tag=tag, align_bytes=64)
 
+        def placed(name, shape, dtype, offset):
+            return reuse.tile(shape, dtype, name=name, offset=offset, align_bytes=64)
+
         def bank(number, shape):
             return psum.tile(shape, F32, name="acc", tag=f"bank{number}")
 
         x_word = sb("x_word", [P, T], U32)
         x_scale = sb("x_scale", [P, T], U8)
         w1_raw = sb("w1_raw", [P, N], U32)
-        w2_raw = sb("w2_raw", [P, N], U32)
+        w2_raw = sb("w2_raw", [P, N], U32, "w2_raw_slot")
         w4_raw = sb("w4_raw", [P, N], U32)
         w1_scale_raw = sb("w1_scale_raw", [P, N], U8)
         w4_scale_raw = sb("w4_scale_raw", [P, N], U8)
-        w2_scale_raw = sb("w2_scale_raw", [P, N], U8, "w2_scale_slot")
+        w2_scale_raw = sb("w2_scale_raw", [P, N], U8)
         w3_raw = [sb(f"w3_raw{n}", [P, PACK, hi - lo], F32, f"w3_slot{n}") for n, (lo, hi) in enumerate(W3_PARTS)]
         warm = sb("warm", [P, 8], F32)
         warm_out = sb("warm_out", [P, 8], F32)
@@ -133,9 +137,9 @@ def tile_picked_zdin_sigmoid_po_kernel(
         hist_word = sb("hist_word", [P, S], U32)
         nc.vector.tensor_copy(out=hist_word[:], in_=x_word[:].indirect(offs_sb[:]))
         deal(nc.vector.tensor_copy, w2_scale, w2_scale_raw, LINE)
-        tgt_word = sb("tgt_word", [P, V], U32, "w2_scale_slot")
-        nc.vector.tensor_copy(out=tgt_word[:], in_=x_word[:].indirect(tgt_sb[:]))
         deal(nc.scalar.copy, w2_word, w2_raw, LINE // 4)
+        tgt_word = sb("tgt_word", [P, V], U32, "w2_raw_slot")
+        nc.vector.tensor_copy(out=tgt_word[:], in_=x_word[:].indirect(tgt_sb[:]))
         deal(nc.scalar.copy, w1_word, w1_raw, LINE // 4)
         deal(nc.vector.tensor_copy, w1_scale, w1_scale_raw, LINE)
 
@@ -163,7 +167,7 @@ def tile_picked_zdin_sigmoid_po_kernel(
         def rows_of(word, scale, t, number, name):
             acc = bank(number, [P, S])
             product(acc[:], word[:, block(t)], scale[:, block(t)], hist_word[:], hist_scale[:])
-            rows = sb(name, [P, S], F32)
+            rows = sb(name, [P, S], F32, name)
             nc.scalar.copy(out=rows[:], in_=acc[:])
             return rows
 
@@ -174,10 +178,13 @@ def tile_picked_zdin_sigmoid_po_kernel(
             targets.append(bank([2, 3, 5, 4][t], [P, V]))
             product(targets[t][:], w1_word[:, block(t)], w1_scale[:, block(t)], tgt_word[:], tgt_scale[:])
         for t in range(TILES):
-            e_sb = sb(f"e_sb{t}", [P, S], F32, ["w3_slot1", "w2_scale_slot", "", ""][t])
+            e_sb = sb(f"e_sb{t}", [P, S], F32, ["w3_slot1", "w2_raw_slot", "", ""][t])
             nc.scalar.copy(out=e_sb[:], in_=(keys_acc[t] if t < 2 else key_product(t))[:])
             y_acc = targets[t]
-            logit.append(sb(f"logit{t}", [P, 2, V], F32, "last_logits" if t == LAST else ""))
+            if t < LAST:
+                logit.append(sb(f"logit{t}", [P, 2, V], F32, f"logit_slot{t}"))
+            else:
+                logit.append(placed("last_logit", [P, 2, V], F32, 0))
             if t < LAST:
                 y_sb = sb(f"y_sb{t}", [P, V], F32)
                 nc.scalar.copy(out=y_sb[:], in_=y_acc[:])
@@ -199,28 +206,38 @@ def tile_picked_zdin_sigmoid_po_kernel(
                 )
 
         term = sb("term", [P, 2, TILES, V], F32)
+        h_sb = []
+        gate = []
         for t in range(TILES):
-            h_sb = rows_of(w3_word, w3_scale, t, [6, 7, 0, 1][t], f"h_sb{t}")
-            gate = sb(f"gate{t}", [P, 2, V], F32)
-            nc.scalar.activation(out=gate[:], in_=logit[t][:], func=SIGMOID)
-            for d in range(2 if t < LAST else 1):
+            h_sb.append(rows_of(w3_word, w3_scale, t, [6, 7, 0, 1][t], f"h_sb{t}"))
+            gate.append(sb(f"gate{t}", [P, 2, V], F32))
+            nc.scalar.activation(out=gate[t][:], in_=logit[t][:], func=SIGMOID)
+            width = V if t < 2 else HALF
+            for d in range(2):
                 nc.vector.tensor_tensor(
-                    out=term[:, d, t, :], in0=h_sb[:].indirect(pos_sb[d][:]), in1=gate[:, d, :], op=MULT
+                    out=term[:, d, t, :width], in0=h_sb[t][:].indirect(pos_sb[d][:, : width // 16]),
+                    in1=gate[t][:, d, :width], op=MULT,
                 )
-        picked = sb("picked", [P, V], F32, "picked_slot")
-        nc.scalar.activation(out=picked[:], in_=h_sb[:].indirect(pos_sb[1][:]), func=COPY)
-        for u in range(2):
-            nc.vector.tensor_tensor(
-                out=term[:, 1, LAST, block(u)], in0=picked[:, block(u)], in1=gate[:, 1, block(u)], op=MULT
-            )
-        w4_word = sb("w4_word", [P, N], U32, "last_logits")
+            if t == 2:
+                w4_scale = sb("w4_scale", [P, N], U8, "logit_slot2")
+                deal(nc.vector.tensor_copy, w4_scale, w4_scale_raw, LINE)
+        picked = {LAST: sb("picked3", [P, 2, HALF], F32), 2: placed("picked2", [P, 2, HALF], F32, 0)}
+        for t in picked:
+            for d in range(2):
+                nc.scalar.activation(out=picked[t][:, d, :], in_=h_sb[t][:].indirect(half_of(pos_sb[d], 1)), func=COPY)
+        w4_word = placed("w4_word", [P, N], U32, 8 * HALF)
         deal(nc.scalar.copy, w4_word, w4_raw, LINE // 4)
+
+        def weigh_picked(t):
+            nc.vector.tensor_tensor(out=term[:, :, t, HALF:], in0=picked[t][:], in1=gate[t][:, :, HALF:], op=MULT)
+
+        weigh_picked(LAST)
 
         out_rows = out_0.rearrange("(p t) v -> p t v", t=PACK)
         out_words = out_1[0].rearrange("p v t -> p (v t)").bitcast(I32)
         out_scale = sb("out_scale", [P, V], U8)
-        z_bf = [sb(f"z_bf{u}", [P, HALF, PACK], BF16) for u in range(2)]
-        z_word = [sb(f"z_word{u}", [P, HALF], U32) for u in range(2)]
+        z_bf = [sb(f"z_bf{u}", [P, HALF, PACK], BF16, "h_sb3" if u == 0 else "") for u in range(2)]
+        z_word = [sb(f"z_word{u}", [P, HALF], U32, "h_sb2" if u == 0 else "") for u in range(2)]
         z_scale = [sb(f"z_scale{u}", [P, HALF], U8) for u in range(2)]
         out_sb = [sb(f"out_sb{u}", [P, PACK, HALF], F32) for u in range(2)]
         out_bf = [sb(f"out_bf{u}", [P, HALF, PACK], BF16) for u in range(2)]
@@ -233,8 +250,7 @@ def tile_picked_zdin_sigmoid_po_kernel(
                 op=ADD,
             )
             if u == 0:
-                w4_scale = sb("w4_scale", [P, N], U8, "picked_slot")
-                deal(nc.vector.tensor_copy, w4_scale, w4_scale_raw, LINE)
+                weigh_picked(2)
             nc.vector.quantize_mx(
                 out=z_word[u][:].bitcast(FP8X4), scales=z_scale[u][:], in_=z_bf[u][:].rearrange("p v t -> p (v t)")
             )

@@ -24,7 +24,7 @@ TILES = 4
 LAST = TILES - 1
 HALF = V // 2
 LINE = 16
-W3_PARTS = [(0, 128), (128, 256), (256, 512)]
+W3_PARTS = [(0, 128), (128, 256), (256, 384), (384, 512)]
 
 
 def block(n):
@@ -121,10 +121,12 @@ def tile_picked_zdin_sigmoid_po_kernel(
         load_w3(1)
         load_repeated(nc.sync, w1_scale_raw, w1_scales, LAST)
         load_w3(2)
+        load_w3(3)
         nc.sync.dma_start(pos_sb[0][:], pos1)
         nc.sync.dma_start(pos_sb[1][:], pos2)
         load_words(nc.sync, w4_raw, w4_words)
-        load_scales(nc.sync, w4_scale_raw, w4_scales)
+        load_scales(nc.sync, w4_scale_raw, w4_scales, range(LAST))
+        load_scales(nc.gpsimd, w4_scale_raw, w4_scales, range(LAST, QUADS))
 
         hist_scale = sb("hist_scale", [P, S], U8)
         tgt_scale = sb("tgt_scale", [P, V], U8)
@@ -152,15 +154,19 @@ def tile_picked_zdin_sigmoid_po_kernel(
         w3_bf = sb("w3_bf", [P, TILES, P, PACK], BF16)
         w3_word = sb("w3_word", [P, H], U32)
         w3_scale = sb("w3_scale", [P, H], U8)
-        for n, copy in enumerate([nc.scalar.copy, nc.scalar.copy, nc.vector.tensor_copy]):
+
+        def round_w3(n, copy):
             lo, hi = W3_PARTS[n]
             copy(
                 out=w3_bf[:, :, lo // PACK : hi // PACK, :].rearrange("p t (c i) j -> p c j i t", i=2),
                 in_=w3_raw[n][:].rearrange("p j (c i t) -> p c j i t", i=2, t=PACK),
             )
 
+        for n, copy in enumerate([nc.scalar.copy, nc.scalar.copy, nc.vector.tensor_copy]):
+            round_w3(n, copy)
+
         def key_product(t):
-            acc = bank(t, [P, S])
+            acc = bank(t % 2, [P, S])
             product(acc[:], w2_word[:, block(t)], w2_scale[:, block(t)], hist_word[:], hist_scale[:])
             return acc
 
@@ -177,9 +183,13 @@ def tile_picked_zdin_sigmoid_po_kernel(
         for t in range(TILES):
             targets.append(bank([2, 3, 5, 4][t], [P, V]))
             product(targets[t][:], w1_word[:, block(t)], w1_scale[:, block(t)], tgt_word[:], tgt_scale[:])
+        e_all = [sb(f"e_sb{t}", [P, S], F32, ["w3_slot1", "w3_slot2", "", ""][t]) for t in range(TILES)]
+        nc.vector.tensor_copy(out=e_all[1][:], in_=keys_acc[1][:])
+        round_w3(3, nc.vector.tensor_copy)
         for t in range(TILES):
-            e_sb = sb(f"e_sb{t}", [P, S], F32, ["w3_slot1", "w2_raw_slot", "", ""][t])
-            nc.scalar.copy(out=e_sb[:], in_=(keys_acc[t] if t < 2 else key_product(t))[:])
+            e_sb = e_all[t]
+            if t != 1:
+                nc.scalar.copy(out=e_sb[:], in_=(keys_acc[t] if t == 0 else key_product(t))[:])
             y_acc = targets[t]
             if t < LAST:
                 logit.append(sb(f"logit{t}", [P, 2, V], F32, f"logit_slot{t}"))
@@ -189,9 +199,13 @@ def tile_picked_zdin_sigmoid_po_kernel(
                 y_sb = sb(f"y_sb{t}", [P, V], F32)
                 nc.scalar.copy(out=y_sb[:], in_=y_acc[:])
                 for d in range(2):
-                    nc.vector.tensor_tensor(
-                        out=logit[t][:, d, :], in0=e_sb[:].indirect(pos_sb[d][:]), in1=y_sb[:], op=MULT
-                    )
+                    if (t, d) == (2, 1):
+                        third_keys = sb("third_keys", [P, V], F32)
+                        nc.scalar.activation(out=third_keys[:], in_=e_sb[:].indirect(pos_sb[d][:]), func=COPY)
+                        key = third_keys[:]
+                    else:
+                        key = e_sb[:].indirect(pos_sb[d][:])
+                    nc.vector.tensor_tensor(out=logit[t][:, d, :], in0=key, in1=y_sb[:], op=MULT)
                     if t == 0 and d == 0:
                         nc.vector.quantize_mx(
                             out=w3_word[:].bitcast(FP8X4), scales=w3_scale[:],
@@ -209,7 +223,7 @@ def tile_picked_zdin_sigmoid_po_kernel(
         h_sb = []
         gate = []
         for t in range(TILES):
-            h_sb.append(rows_of(w3_word, w3_scale, t, [6, 7, 0, 1][t], f"h_sb{t}"))
+            h_sb.append(rows_of(w3_word, w3_scale, t, [6, 7, 2, 3][t], f"h_sb{t}"))
             gate.append(sb(f"gate{t}", [P, 2, V], F32))
             nc.scalar.activation(out=gate[t][:], in_=logit[t][:], func=SIGMOID)
             width = V if t < 2 else HALF
@@ -255,7 +269,7 @@ def tile_picked_zdin_sigmoid_po_kernel(
                 out=z_word[u][:].bitcast(FP8X4), scales=z_scale[u][:], in_=z_bf[u][:].rearrange("p v t -> p (v t)")
             )
             for n in range(2):
-                acc = bank([[2, 3], [5, 6]][u][n], [P, 2, HALF])
+                acc = bank([[0, 1], [5, 6]][u][n], [P, 2, HALF])
                 for s in range(2):
                     cols = block(2 * n + s)
                     product(acc[:, s, :], w4_word[:, cols], w4_scale[:, cols], z_word[u][:], z_scale[u][:])

@@ -87,7 +87,7 @@ def tile_picked_zdin_sigmoid_po_kernel(
 
         x_word = sb("x_word", [P, T], U32)
         x_scale = sb("x_scale", [P, T], U8)
-        w1_raw = sb("w1_raw", [P, N], U32)
+        w1_raw = sb("w1_raw", [P, N], U32, "w1_raw_slot")
         w2_raw = sb("w2_raw", [P, N], U32, "w2_raw_slot")
         w4_raw = sb("w4_raw", [P, N], U32)
         w1_scale_raw = sb("w1_scale_raw", [P, N], U8)
@@ -183,7 +183,7 @@ def tile_picked_zdin_sigmoid_po_kernel(
         for t in range(TILES):
             targets.append(bank([2, 3, 5, 4][t], [P, V]))
             product(targets[t][:], w1_word[:, block(t)], w1_scale[:, block(t)], tgt_word[:], tgt_scale[:])
-        e_all = [sb(f"e_sb{t}", [P, S], F32, ["w3_slot1", "w3_slot2", "", ""][t]) for t in range(TILES)]
+        e_all = [sb(f"e_sb{t}", [P, S], F32, ["w1_raw_slot", "w3_slot2", "", ""][t]) for t in range(TILES)]
         nc.vector.tensor_copy(out=e_all[1][:], in_=keys_acc[1][:])
         round_w3(3, nc.vector.tensor_copy)
         for t in range(TILES):

@@ -89,9 +89,8 @@ def tile_picked_zdin_sigmoid_po_kernel(
         x_scale = sb("x_scale", [P, T], U8)
         w1_raw = sb("w1_raw", [P, N], U32, "w1_raw_slot")
         w2_raw = sb("w2_raw", [P, N], U32, "w2_raw_slot")
-        w4_raw = sb("w4_raw", [P, N], U32)
         w1_scale_raw = sb("w1_scale_raw", [P, N], U8)
-        w4_scale_raw = sb("w4_scale_raw", [P, N], U8)
+        w4_scale_raw = sb("w4_scale_raw", [P, N], U8, "w4_scale_slot")
         w2_scale_raw = sb("w2_scale_raw", [P, N], U8)
         w3_raw = [sb(f"w3_raw{n}", [P, PACK, hi - lo], F32, f"w3_slot{n}") for n, (lo, hi) in enumerate(W3_PARTS)]
         warm = sb("warm", [P, 8], F32)
@@ -121,12 +120,10 @@ def tile_picked_zdin_sigmoid_po_kernel(
         load_w3(1)
         load_repeated(nc.sync, w1_scale_raw, w1_scales, LAST)
         load_w3(2)
+        load_scales(nc.sync, w4_scale_raw, w4_scales)
         load_w3(3)
         nc.sync.dma_start(pos_sb[0][:], pos1)
         nc.sync.dma_start(pos_sb[1][:], pos2)
-        load_words(nc.sync, w4_raw, w4_words)
-        load_scales(nc.sync, w4_scale_raw, w4_scales, range(LAST))
-        load_scales(nc.gpsimd, w4_scale_raw, w4_scales, range(LAST, QUADS))
 
         hist_scale = sb("hist_scale", [P, S], U8)
         tgt_scale = sb("tgt_scale", [P, V], U8)
@@ -165,6 +162,9 @@ def tile_picked_zdin_sigmoid_po_kernel(
         for n, copy in enumerate([nc.scalar.copy, nc.scalar.copy, nc.vector.tensor_copy]):
             round_w3(n, copy)
 
+        w4_scale = sb("w4_scale", [P, N], U8)
+        deal(nc.vector.tensor_copy, w4_scale, w4_scale_raw, LINE)
+
         def key_product(t):
             acc = bank(t % 2, [P, S])
             product(acc[:], w2_word[:, block(t)], w2_scale[:, block(t)], hist_word[:], hist_scale[:])
@@ -183,9 +183,11 @@ def tile_picked_zdin_sigmoid_po_kernel(
         for t in range(TILES):
             targets.append(bank([2, 3, 5, 4][t], [P, V]))
             product(targets[t][:], w1_word[:, block(t)], w1_scale[:, block(t)], tgt_word[:], tgt_scale[:])
-        e_all = [sb(f"e_sb{t}", [P, S], F32, ["w1_raw_slot", "w3_slot2", "", ""][t]) for t in range(TILES)]
+        e_all = [sb(f"e_sb{t}", [P, S], F32, ["w1_raw_slot", "w4_scale_slot", "", ""][t]) for t in range(TILES)]
         nc.vector.tensor_copy(out=e_all[1][:], in_=keys_acc[1][:])
         round_w3(3, nc.vector.tensor_copy)
+        w4_raw = sb("w4_raw", [P, N], U32, "w3_slot3")
+        load_words(nc.gpsimd, w4_raw, w4_words)
         for t in range(TILES):
             e_sb = e_all[t]
             if t != 1:
@@ -194,7 +196,7 @@ def tile_picked_zdin_sigmoid_po_kernel(
             if t < LAST:
                 logit.append(sb(f"logit{t}", [P, 2, V], F32, f"logit_slot{t}"))
             else:
-                logit.append(placed("last_logit", [P, 2, V], F32, 0))
+                logit.append(placed("last_logit", [P, 2, V], F32, 1024))
             if t < LAST:
                 y_sb = sb(f"y_sb{t}", [P, V], F32)
                 nc.scalar.copy(out=y_sb[:], in_=y_acc[:])
@@ -224,26 +226,27 @@ def tile_picked_zdin_sigmoid_po_kernel(
         gate = []
         for t in range(TILES):
             h_sb.append(rows_of(w3_word, w3_scale, t, [6, 7, 2, 3][t], f"h_sb{t}"))
-            gate.append(sb(f"gate{t}", [P, 2, V], F32))
-            nc.scalar.activation(out=gate[t][:], in_=logit[t][:], func=SIGMOID)
+            early = HALF if t == 2 else V
+            gate.append(sb(f"gate{t}", [P, 2, early], F32))
+            nc.scalar.activation(out=gate[t][:], in_=logit[t][:, :, :early], func=SIGMOID)
             width = V if t < 2 else HALF
             for d in range(2):
                 nc.vector.tensor_tensor(
                     out=term[:, d, t, :width], in0=h_sb[t][:].indirect(pos_sb[d][:, : width // 16]),
                     in1=gate[t][:, d, :width], op=MULT,
                 )
-            if t == 2:
-                w4_scale = sb("w4_scale", [P, N], U8, "logit_slot2")
-                deal(nc.vector.tensor_copy, w4_scale, w4_scale_raw, LINE)
-        picked = {LAST: sb("picked3", [P, 2, HALF], F32), 2: placed("picked2", [P, 2, HALF], F32, 0)}
+        picked = {LAST: sb("picked3", [P, 2, HALF], F32), 2: placed("picked2", [P, 2, HALF], F32, 64)}
+        late_gate = {LAST: gate[LAST][:, :, HALF:], 2: placed("late_gate", [P, 2, HALF], F32, 1088)[:]}
         for t in picked:
+            if t == 2:
+                nc.scalar.activation(out=late_gate[t], in_=logit[t][:, :, HALF:], func=SIGMOID)
             for d in range(2):
                 nc.scalar.activation(out=picked[t][:, d, :], in_=h_sb[t][:].indirect(half_of(pos_sb[d], 1)), func=COPY)
-        w4_word = placed("w4_word", [P, N], U32, 8 * HALF)
+        w4_word = placed("w4_word", [P, N], U32, 2112)
         deal(nc.scalar.copy, w4_word, w4_raw, LINE // 4)
 
         def weigh_picked(t):
-            nc.vector.tensor_tensor(out=term[:, :, t, HALF:], in0=picked[t][:], in1=gate[t][:, :, HALF:], op=MULT)
+            nc.vector.tensor_tensor(out=term[:, :, t, HALF:], in0=picked[t][:], in1=late_gate[t], op=MULT)
 
         weigh_picked(LAST)
 

@@ -148,7 +148,7 @@ def tile_picked_zdin_sigmoid_po_kernel(
                 rhs=rhs_word.bitcast(FP8X4), rhs_scale=rhs_scale, start=True, stop=True,
             )
 
-        w3_bf = sb("w3_bf", [P, TILES, P, PACK], BF16)
+        w3_bf = sb("w3_bf", [P, TILES, P, PACK], BF16, "w3_bf_slot")
         w3_word = sb("w3_word", [P, H], U32)
         w3_scale = sb("w3_scale", [P, H], U8)
 
@@ -180,18 +180,22 @@ def tile_picked_zdin_sigmoid_po_kernel(
         logit = []
         keys_acc = [key_product(t) for t in range(2)]
         targets = []
-        for t in range(TILES):
-            targets.append(bank([2, 3, 5, 4][t], [P, V]))
+
+        def target_product(t):
+            targets.append(bank([2, 3, 5, 2][t], [P, V]))
             product(targets[t][:], w1_word[:, block(t)], w1_scale[:, block(t)], tgt_word[:], tgt_scale[:])
+
+        for t in range(LAST):
+            target_product(t)
         e_all = [sb(f"e_sb{t}", [P, S], F32, ["w1_raw_slot", "w4_scale_slot", "", ""][t]) for t in range(TILES)]
         nc.vector.tensor_copy(out=e_all[1][:], in_=keys_acc[1][:])
         round_w3(3, nc.vector.tensor_copy)
-        w4_raw = sb("w4_raw", [P, N], U32, "w3_slot3")
-        load_words(nc.gpsimd, w4_raw, w4_words)
         for t in range(TILES):
             e_sb = e_all[t]
             if t != 1:
                 nc.scalar.copy(out=e_sb[:], in_=(keys_acc[t] if t == 0 else key_product(t))[:])
+            if t == LAST:
+                target_product(t)
             y_acc = targets[t]
             if t < LAST:
                 logit.append(sb(f"logit{t}", [P, 2, V], F32, f"logit_slot{t}"))
@@ -221,11 +225,13 @@ def tile_picked_zdin_sigmoid_po_kernel(
                     out=logit[t][:], in0=keys[:], in1=y_acc[:].unsqueeze(1).broadcast_to([P, 2, V]), op=MULT
                 )
 
+        w4_raw = sb("w4_raw", [P, N], U32, "w3_bf_slot")
+        load_words(nc.gpsimd, w4_raw, w4_words)
         term = sb("term", [P, 2, TILES, V], F32)
         h_sb = []
         gate = []
         for t in range(TILES):
-            h_sb.append(rows_of(w3_word, w3_scale, t, [6, 7, 2, 3][t], f"h_sb{t}"))
+            h_sb.append(rows_of(w3_word, w3_scale, t, [6, 7, 4, 3][t], f"h_sb{t}"))
             early = HALF if t == 2 else V
             gate.append(sb(f"gate{t}", [P, 2, early], F32))
             nc.scalar.activation(out=gate[t][:], in_=logit[t][:, :, :early], func=SIGMOID)

from contextlib import ExitStack

import concourse.mybir as mybir

K, T, S, V, H, N = 512, 1024, 512, 256, 512, 512
FLOPS = 2 * K * (N * V + N * S + H * S) + 2 * H * N * V

F32 = mybir.dt.float32
BF16 = mybir.dt.bfloat16
I32 = mybir.dt.int32
U32 = mybir.dt.uint32
U16 = mybir.dt.uint16
U8 = mybir.dt.uint8
FP8X4 = mybir.dt.float8_e4m3fn_x4
MULT = mybir.AluOpType.mult
ADD = mybir.AluOpType.add
SIGMOID = mybir.ActivationFunctionType.Sigmoid
COPY = mybir.ActivationFunctionType.Copy

P = 128
PACK = 4
QUADS = 4
TILES = 4
LAST = TILES - 1
HALF = V // 2
LINE = 16
W3_PARTS = [(0, 128), (128, 256), (256, 384), (384, 512)]


def block(n):
    return slice(P * n, P * (n + 1))


def half_of(offsets, u):
    return offsets[:, u * HALF // 16 : (u + 1) * HALF // 16]


def load_words(queue, tile, words):
    queue.dma_start(out=tile[:].bitcast(I32), in_=words[0].rearrange("p n t -> p (n t)").bitcast(I32))


def load_scales(queue, tile, scales, quads=range(QUADS)):
    for q in quads:
        queue.dma_start(
            out=tile[32 * q : 32 * q + 4, :].bitcast(I32),
            in_=scales[0, 4 * q : 4 * q + 4, :].bitcast(I32),
        )


def load_repeated(queue, tile, scales, q):
    rows = scales[0, 4 * q : 4 * q + 4, :].bitcast(I32)
    queue.dma_start(
        out=tile[32 * q : 32 * (q + 1), :].bitcast(I32), in_=rows.unsqueeze(0).broadcast_to([8, 4, rows.shape[1]])
    )


def deal(copy, dealt, raw, run):
    copy(
        out=dealt[:].rearrange("p (t c i) -> p c t i", t=PACK, i=run),
        in_=raw[:].rearrange("p (c i t) -> p c t i", t=PACK, i=run),
    )


def tile_picked_zdin_sigmoid_po_kernel(
    tc, x_words, x_scales, w1_words, w1_scales, w2_words, w2_scales, w3, w4_words, w4_scales,
    offs, tgt, pos1, pos2, out_0, out_1, out_2,
):
    nc = tc.nc
    with ExitStack() as ctx:
        lists = ctx.enter_context(tc.tile_pool(name="lists", bufs=1))
        keep = ctx.enter_context(tc.tile_pool(name="keep", bufs=1))
        reuse = ctx.enter_context(tc.tile_pool(name="reuse", bufs=1))
        psum = ctx.enter_context(tc.psum_pool(name="psum", bufs=1))

        offs_sb = lists.tile([P, S // 16], U16, name="offs_sb")
        tgt_sb = lists.tile([P, V // 16], U16, name="tgt_sb")
        pos_sb = [lists.tile([P, V // 16], U16, name=f"pos_sb{d}") for d in range(2)]

        def sb(name, shape, dtype, tag=""):
            return keep.tile(shape, dtype, name=name, tag=tag, align_bytes=64)

        def placed(name, shape, dtype, offset):
            return reuse.tile(shape, dtype, name=name, offset=offset, align_bytes=64)

        def bank(number, shape):
            return psum.tile(shape, F32, name="acc", tag=f"bank{number}")

        x_word = sb("x_word", [P, T], U32)
        x_scale = sb("x_scale", [P, T], U8)
        w1_raw = sb("w1_raw", [P, N], U32, "w1_raw_slot")
        w2_raw = sb("w2_raw", [P, N], U32, "w2_raw_slot")
        w1_scale_raw = sb("w1_scale_raw", [P, N], U8)
        w4_scale_raw = sb("w4_scale_raw", [P, N], U8, "w4_scale_slot")
        w2_scale_raw = sb("w2_scale_raw", [P, N], U8)
        w3_raw = [sb(f"w3_raw{n}", [P, PACK, hi - lo], F32, f"w3_slot{n}") for n, (lo, hi) in enumerate(W3_PARTS)]
        warm = sb("warm", [P, 8], F32)
        warm_out = sb("warm_out", [P, 8], F32)

        for q in range(LAST):
            load_repeated(nc.gpsimd, w1_scale_raw, w1_scales, q)
        nc.vector.memset(warm[:], 0.0)
        nc.vector.memset(w2_scale_raw[:].bitcast(I32), 0)
        nc.vector.memset(w4_scale_raw[:].bitcast(I32), 0)

        w3_rows = w3.rearrange("(p j) c -> p j c", j=PACK)
        nc.sync.dma_start(offs_sb[:], offs)
        for q in range(QUADS):
            load_repeated(nc.sync if q < QUADS // 2 else nc.scalar, x_scale, x_scales, q)
        nc.scalar.activation(out=warm_out[:], in_=warm[:], func=SIGMOID)

        def load_w3(n):
            nc.sync.dma_start(out=w3_raw[n][:], in_=w3_rows[:, :, W3_PARTS[n][0] : W3_PARTS[n][1]])

        nc.sync.dma_start(tgt_sb[:], tgt)
        load_w3(0)
        load_words(nc.sync, x_word, x_words)
        load_scales(nc.sync, w2_scale_raw, w2_scales)
        load_words(nc.sync, w2_raw, w2_words)
        load_words(nc.sync, w1_raw, w1_words)
        load_w3(1)
        load_repeated(nc.sync, w1_scale_raw, w1_scales, LAST)
        load_w3(2)
        load_scales(nc.sync, w4_scale_raw, w4_scales)
        load_w3(3)
        nc.sync.dma_start(pos_sb[0][:], pos1)
        nc.sync.dma_start(pos_sb[1][:], pos2)

        hist_scale = sb("hist_scale", [P, S], U8)
        tgt_scale = sb("tgt_scale", [P, V], U8)
        w1_word = sb("w1_word", [P, N], U32)
        w2_word = sb("w2_word", [P, N], U32)
        w1_scale = sb("w1_scale", [P, N], U8)
        w2_scale = sb("w2_scale", [P, N], U8)
        nc.vector.tensor_copy(out=hist_scale[:], in_=x_scale[:].indirect(offs_sb[:]))
        nc.vector.tensor_copy(out=tgt_scale[:], in_=x_scale[:].indirect(tgt_sb[:]))
        hist_word = sb("hist_word", [P, S], U32)
        nc.vector.tensor_copy(out=hist_word[:], in_=x_word[:].indirect(offs_sb[:]))
        deal(nc.vector.tensor_copy, w2_scale, w2_scale_raw, LINE)
        deal(nc.scalar.copy, w2_word, w2_raw, LINE // 4)
        tgt_word = sb("tgt_word", [P, V], U32, "w2_raw_slot")
        nc.vector.tensor_copy(out=tgt_word[:], in_=x_word[:].indirect(tgt_sb[:]))
        deal(nc.scalar.copy, w1_word, w1_raw, LINE // 4)
        deal(nc.vector.tensor_copy, w1_scale, w1_scale_raw, LINE)

        def product(acc, word, scale, rhs_word, rhs_scale):
            nc.tensor.matmul_mx(
                out=acc, lhsT=word.bitcast(FP8X4), lhsT_scale=scale,
                rhs=rhs_word.bitcast(FP8X4), rhs_scale=rhs_scale, start=True, stop=True,
            )

        w3_bf = sb("w3_bf", [P, TILES, P, PACK], BF16, "w3_bf_slot")
        w3_word = sb("w3_word", [P, H], U32)
        w3_scale = sb("w3_scale", [P, H], U8)

        def round_w3(n, copy):
            lo, hi = W3_PARTS[n]
            copy(
                out=w3_bf[:, :, lo // PACK : hi // PACK, :].rearrange("p t (c i) j -> p c j i t", i=2),
                in_=w3_raw[n][:].rearrange("p j (c i t) -> p c j i t", i=2, t=PACK),
            )

        for n, copy in enumerate([nc.scalar.copy, nc.scalar.copy, nc.vector.tensor_copy]):
            round_w3(n, copy)

        w4_scale = sb("w4_scale", [P, N], U8)
        deal(nc.vector.tensor_copy, w4_scale, w4_scale_raw, LINE)

        def key_product(t):
            acc = bank(t % 2, [P, S])
            product(acc[:], w2_word[:, block(t)], w2_scale[:, block(t)], hist_word[:], hist_scale[:])
            return acc

        def rows_of(word, scale, t, number, name):
            acc = bank(number, [P, S])
            product(acc[:], word[:, block(t)], scale[:, block(t)], hist_word[:], hist_scale[:])
            rows = sb(name, [P, S], F32, name)
            nc.scalar.copy(out=rows[:], in_=acc[:])
            return rows

        logit = []
        keys_acc = [key_product(t) for t in range(2)]
        targets = []

        def target_product(t):
            targets.append(bank([2, 3, 5, 2][t], [P, V]))
            product(targets[t][:], w1_word[:, block(t)], w1_scale[:, block(t)], tgt_word[:], tgt_scale[:])

        for t in range(LAST):
            target_product(t)
        e_all = [sb(f"e_sb{t}", [P, S], F32, ["w1_raw_slot", "w4_scale_slot", "", ""][t]) for t in range(TILES)]
        nc.vector.tensor_copy(out=e_all[1][:], in_=keys_acc[1][:])
        round_w3(3, nc.vector.tensor_copy)
        for t in range(TILES):
            e_sb = e_all[t]
            if t != 1:
                nc.scalar.copy(out=e_sb[:], in_=(keys_acc[t] if t == 0 else key_product(t))[:])
            if t == LAST:
                target_product(t)
            y_acc = targets[t]
            if t < LAST:
                logit.append(sb(f"logit{t}", [P, 2, V], F32, f"logit_slot{t}"))
            else:
                logit.append(placed("last_logit", [P, 2, V], F32, 1024))
            if t < LAST:
                y_sb = sb(f"y_sb{t}", [P, V], F32)
                nc.scalar.copy(out=y_sb[:], in_=y_acc[:])
                for d in range(2):
                    if (t, d) == (2, 1):
                        third_keys = sb("third_keys", [P, V], F32)
                        nc.scalar.activation(out=third_keys[:], in_=e_sb[:].indirect(pos_sb[d][:]), func=COPY)
                        key = third_keys[:]
                    else:
                        key = e_sb[:].indirect(pos_sb[d][:])
                    nc.vector.tensor_tensor(out=logit[t][:, d, :], in0=key, in1=y_sb[:], op=MULT)
                    if t == 0 and d == 0:
                        nc.vector.quantize_mx(
                            out=w3_word[:].bitcast(FP8X4), scales=w3_scale[:],
                            in_=w3_bf[:].rearrange("p t m j -> p (t m j)"),
                        )
            else:
                keys = sb("keys", [P, 2, V], F32)
                for d in range(2):
                    nc.scalar.activation(out=keys[:, d, :], in_=e_sb[:].indirect(pos_sb[d][:]), func=COPY)
                nc.vector.tensor_tensor(
                    out=logit[t][:], in0=keys[:], in1=y_acc[:].unsqueeze(1).broadcast_to([P, 2, V]), op=MULT
                )

        w4_raw = sb("w4_raw", [P, N], U32, "w3_bf_slot")
        load_words(nc.gpsimd, w4_raw, w4_words)
        term = sb("term", [P, 2, TILES, V], F32)
        h_sb = []
        gate = []
        for t in range(TILES):
            h_sb.append(rows_of(w3_word, w3_scale, t, [6, 7, 4, 3][t], f"h_sb{t}"))
            early = HALF if t == 2 else V
            gate.append(sb(f"gate{t}", [P, 2, early], F32))
            nc.scalar.activation(out=gate[t][:], in_=logit[t][:, :, :early], func=SIGMOID)
            width = V if t < 2 else HALF
            for d in range(2):
                nc.vector.tensor_tensor(
                    out=term[:, d, t, :width], in0=h_sb[t][:].indirect(pos_sb[d][:, : width // 16]),
                    in1=gate[t][:, d, :width], op=MULT,
                )
        picked = {LAST: sb("picked3", [P, 2, HALF], F32), 2: placed("picked2", [P, 2, HALF], F32, 64)}
        late_gate = {LAST: gate[LAST][:, :, HALF:], 2: placed("late_gate", [P, 2, HALF], F32, 1088)[:]}
        for t in picked:
            if t == 2:
                nc.scalar.activation(out=late_gate[t], in_=logit[t][:, :, HALF:], func=SIGMOID)
            for d in range(2):
                nc.scalar.activation(out=picked[t][:, d, :], in_=h_sb[t][:].indirect(half_of(pos_sb[d], 1)), func=COPY)
        w4_word = placed("w4_word", [P, N], U32, 2112)
        deal(nc.scalar.copy, w4_word, w4_raw, LINE // 4)

        def weigh_picked(t):
            nc.vector.tensor_tensor(out=term[:, :, t, HALF:], in0=picked[t][:], in1=late_gate[t], op=MULT)

        weigh_picked(LAST)

        out_rows = out_0.rearrange("(p t) v -> p t v", t=PACK)
        out_words = out_1[0].rearrange("p v t -> p (v t)").bitcast(I32)
        out_scale = sb("out_scale", [P, V], U8)
        z_bf = [sb(f"z_bf{u}", [P, HALF, PACK], BF16, "h_sb3" if u == 0 else "") for u in range(2)]
        z_word = [sb(f"z_word{u}", [P, HALF], U32, "h_sb2" if u == 0 else "") for u in range(2)]
        z_scale = [sb(f"z_scale{u}", [P, HALF], U8) for u in range(2)]
        out_sb = [sb(f"out_sb{u}", [P, PACK, HALF], F32) for u in range(2)]
        out_bf = [sb(f"out_bf{u}", [P, HALF, PACK], BF16) for u in range(2)]
        out_word = [sb(f"out_word{u}", [P, HALF], U32) for u in range(2)]
        for u in range(2):
            nc.vector.tensor_tensor(
                out=z_bf[u][:].rearrange("p (c i) j -> p c j i", i=4),
                in0=term[:, 0, :, block(u)].rearrange("p j (c i) -> p c j i", i=4),
                in1=term[:, 1, :, block(u)].rearrange("p j (c i) -> p c j i", i=4),
                op=ADD,
            )
            if u == 0:
                weigh_picked(2)
            nc.vector.quantize_mx(
                out=z_word[u][:].bitcast(FP8X4), scales=z_scale[u][:], in_=z_bf[u][:].rearrange("p v t -> p (v t)")
            )
            for n in range(2):
                acc = bank([[0, 1], [5, 6]][u][n], [P, 2, HALF])
                for s in range(2):
                    cols = block(2 * n + s)
                    product(acc[:, s, :], w4_word[:, cols], w4_scale[:, cols], z_word[u][:], z_scale[u][:])
                nc.scalar.copy(out=out_sb[u][:, 2 * n : 2 * (n + 1), :], in_=acc[:])
            nc.sync.dma_start(out=out_rows[:, :, block(u)], in_=out_sb[u][:])
        for u in range(2):
            nc.vector.tensor_copy(
                out=out_bf[u][:].rearrange("p (c i) j -> p c j i", i=4),
                in_=out_sb[u][:].rearrange("p j (c i) -> p c j i", i=4),
            )
            nc.vector.quantize_mx(
                out=out_word[u][:].bitcast(FP8X4), scales=out_scale[:, block(u)],
                in_=out_bf[u][:].rearrange("p v t -> p (v t)"),
            )
            nc.sync.dma_start(out=out_words[:, block(u)], in_=out_word[u][:].bitcast(I32))
        for q in range(QUADS):
            queue = nc.sync if q % 2 == 0 else nc.scalar
            queue.dma_start(
                out=out_2[0, 4 * q : 4 * q + 4, :].bitcast(I32), in_=out_scale[32 * q : 32 * q + 4, :].bitcast(I32)
            )
